import numpy as np
import ml_dtypes


def mxq(x, axis, fmt="e4m3"):
    dtype, down = {"e4m3": (ml_dtypes.float8_e4m3fn, 7), "e5m2": (ml_dtypes.float8_e5m2, 14)}[fmt]
    v = np.moveaxis(np.asarray(x, np.float32).astype(ml_dtypes.bfloat16).astype(np.float64), axis, -1)
    blocks = v.reshape(v.shape[:-1] + (-1, 32))
    amax = np.abs(blocks).max(-1, keepdims=True)
    byte = np.maximum(np.where(amax > 0, np.frexp(amax)[1] - 1 + 127, 0) - down, 1)
    scale = np.exp2(byte - 127.0)
    codes = (blocks / scale).astype(np.float32).astype(dtype).astype(np.float64)
    return np.moveaxis((codes * scale).reshape(v.shape), -1, axis)


WIDE = False


def mx_kscale(k):
    if not WIDE:
        return np.ones(k)
    levels = np.array([30, -30])
    if k % 512:
        return np.exp2(np.random.permutation(np.resize(levels, k // 32))).repeat(32)
    a = np.empty((k // 512, 16))
    for p in range(k // 512):
        a[p, :8] = np.random.permutation(np.resize(levels, 8))
        for g in range(8):
            far = levels[np.abs(levels - a[p, g]) >= 10]
            a[p, g + 8] = far[np.random.randint(len(far))]
    return np.exp2(a.ravel()).repeat(32)


def f64(x):
    return np.asarray(x).astype(np.float64)


def striped(idx):
    return np.tile(idx.reshape(-1, 16).T, (8, 1)).astype(np.uint16)


def unstriped(offs):
    return offs[:16].T.reshape(-1).astype(np.int64)


def bf(x):
    return np.asarray(x, np.float32).astype(ml_dtypes.bfloat16)


E2M1 = np.array([0.0, 0.5, 1.0, 1.5, 2.0, 3.0, 4.0, 6.0, -0.0, -0.5, -1.0, -1.5, -2.0, -3.0, -4.0, -6.0])


def pack_weight(w, fmt):
    k, n = w.shape
    w = f64(bf(w)).reshape(k // 32, 32, n)
    amax = np.abs(w).max(1)
    if fmt in ("e4m3", "e5m2"):
        byte = np.frexp(amax)[1] - 1 + 127 - (7 if fmt == "e4m3" else 14)
    else:
        mant, ex = np.frexp(amax / 6.0)
        byte = np.where(mant > 0.5, ex, ex - 1) + 127
    byte = np.clip(np.where(amax > 0, byte, 1), 1, 254)
    scaled = (w * np.exp2(127.0 - byte)[:, None, :]).reshape(k, n).astype(np.float32)
    by_word = np.ascontiguousarray(scaled.reshape(k // 512, 128, 4, n).transpose(0, 1, 3, 2))
    if fmt in ("e4m3", "e5m2"):
        words = by_word.astype(ml_dtypes.float8_e4m3fn if fmt == "e4m3" else ml_dtypes.float8_e5m2).view(np.uint8)
    else:
        c = by_word.astype(ml_dtypes.float4_e2m1fn).view(np.uint8) & 0xF
        words = c[..., 0::2] | (c[..., 1::2] << 4)
    return np.ascontiguousarray(words), np.ascontiguousarray(byte.astype(np.uint8).reshape(k // 512, 16, n))


def unpack_weight(words, scales, fmt):
    g, p, n, _ = words.shape
    if fmt in ("e4m3", "e5m2"):
        vals = np.ascontiguousarray(words).view(ml_dtypes.float8_e4m3fn if fmt == "e4m3" else ml_dtypes.float8_e5m2).astype(np.float64)
    else:
        nib = np.empty((g, p, n, 4), np.uint8)
        nib[..., 0::2] = words & 0xF
        nib[..., 1::2] = words >> 4
        vals = E2M1[nib]
    vals = vals * np.repeat(np.exp2(scales.astype(np.float64) - 127.0), 8, axis=1)[..., None]
    return vals.transpose(0, 1, 3, 2).reshape(g * 512, n)


K, T, S, H, N = 1024, 2048, 1024, 512, 1024

def setup_inputs():
    n = np.random.standard_normal
    s = mx_kscale(K)[:, None]
    u = mx_kscale(H)[:, None]
    grads = n((K, T)) * np.exp(1.0 * n((1, T))) * s
    tab_words, tab_scales = pack_weight(grads, "e5m2")
    w2_words, w2_scales = pack_weight(n((H, N)) / np.sqrt(H) / u, "e4m3")
    return {
        "tab_words": tab_words,
        "tab_scales": tab_scales,
        "offs": striped(np.random.permutation(T)[:S]),
        "w1": (n((K, H)) / np.sqrt(K) / s).astype(np.float32),
        "b1": (0.5 * n(H)).astype(np.float32),
        "gain": (np.exp(0.3 * n(H)) * u[:, 0]).astype(np.float32),
        "w2_words": w2_words,
        "w2_scales": w2_scales,
        "step": np.exp(0.3 * n(N)).astype(np.float32),
        "drift": (0.3 * n(N)).astype(np.float32),
    }

def reference(tab_words, tab_scales, offs, w1, b1, gain, w2_words, w2_scales, step, drift):
    v = unpack_weight(tab_words, tab_scales, "e5m2")[:, unstriped(offs)]
    w1q = mxq(f64(w1), 0, "e4m3")
    a = (w1q.T @ v) + f64(b1)[:, None]
    h = f64(gain)[:, None] * np.tanh(a)
    hq = mxq(h, 0, "e4m3")
    w2 = unpack_weight(w2_words, w2_scales, "e4m3")
    y = w2.T @ hq
    return f64(step)[:, None] * y + f64(drift)[:, None]

@@ -1,0 +1,201 @@
+from contextlib import ExitStack
+
+import concourse.mybir as mybir
+from concourse.masks import make_identity
+
+K, T, S, H, N = 1024, 2048, 1024, 512, 1024
+FLOPS = 2 * K * H * S + 2 * H * N * S
+
+F32 = mybir.dt.float32
+BF16 = mybir.dt.bfloat16
+I32 = mybir.dt.int32
+U32 = mybir.dt.uint32
+U16 = mybir.dt.uint16
+U8 = mybir.dt.uint8
+E4M3 = mybir.dt.float8_e4m3fn_x4
+E5M2 = mybir.dt.float8_e5m2_x4
+ALU = mybir.AluOpType
+ACT = mybir.ActivationFunctionType
+
+P = 128
+PACK = 4
+K_PASS = P * PACK
+BLOCK = 512
+CHUNKS = [(0, 256), (256, 256), (512, 256), (768, 256)]
+N_TILES = N // P
+
+
+def tile_list_federated_client_updates_kernel(
+    tc, tab_words, tab_scales, offs, w1, b1, gain, w2_words, w2_scales, step, drift, out
+):
+    nc = tc.nc
+    with ExitStack() as ctx:
+        held = ctx.enter_context(tc.tile_pool(name="held", bufs=1))
+        shared = ctx.enter_context(tc.tile_pool(name="shared", bufs=1))
+        psum = ctx.enter_context(tc.psum_pool(name="psum", bufs=1))
+
+        offsets = held.tile([P, S // 16], U16, name="offsets")
+        nc.sync.dma_start(offsets[:], offs)
+
+        b1_sb = held.tile([P, PACK], F32, name="b1_sb")
+        gain_sb = held.tile([P, PACK], F32, name="gain_sb")
+
+        w1_raw = [held.tile([P, PACK, H], F32, name=f"w1_raw{a}") for a in range(2)]
+        tab = [held.tile([P, T], I32, name=f"tab{a}", tag=f"tab{a}", align_bytes=64) for a in range(2)]
+
+        def load_w1(a):
+            rows = w1[K_PASS * a : K_PASS * (a + 1), :]
+            nc.sync.dma_start(w1_raw[a][:], rows.rearrange("(p j) c -> p j c", j=PACK))
+
+        def load_table(a):
+            nc.sync.dma_start(tab[a][:], tab_words[a].rearrange("p t i -> p (t i)").bitcast(I32))
+
+        load_w1(0)
+        scale_window = shared.tile([P, T], U8, name="scale_window", align_bytes=64, offset=0)
+        nc.gpsimd.memset(scale_window[:].bitcast(I32), 0)
+        for q in range(4):
+            nc.sync.dma_start(
+                scale_window[32 * q : 32 * q + 8, :].bitcast(I32),
+                tab_scales[:, 4 * q : 4 * q + 4, :].bitcast(I32),
+            )
+        rows_sb = held.tile([P, P], F32, name="rows_sb")
+        ident = held.tile([P, P], F32, name="ident")
+        nc.gpsimd.memset(rows_sb[:], 0.0)
+        load_table(0)
+        load_w1(1)
+        load_table(1)
+        nc.sync.dma_start(rows_sb[0:N_TILES, :], step.rearrange("(b p) -> b p", p=P))
+        nc.sync.dma_start(rows_sb[N_TILES : 2 * N_TILES, :], drift.rearrange("(b p) -> b p", p=P))
+        nc.sync.dma_start(b1_sb[:], b1.rearrange("(p t) -> p t", t=PACK))
+        nc.sync.dma_start(gain_sb[:], gain.rearrange("(p t) -> p t", t=PACK))
+
+        make_identity(nc, ident[:])
+
+        picked_scales = [held.tile([P, S], U8, name=f"picked_scales{a}", align_bytes=64) for a in range(2)]
+        nc.gpsimd.memset(picked_scales[1][:].bitcast(I32), 0)
+        nc.vector.tensor_copy(picked_scales[0][:], scale_window[:].indirect(offsets[:]))
+        nc.sync.dma_start(picked_scales[1][0:100, :].bitcast(I32), picked_scales[0][4:104, :].bitcast(I32))
+
+        w2_plane = shared.tile([P, N], U8, name="w2_plane", align_bytes=64, offset=0)
+        w2_codes = shared.tile([P, N], I32, name="w2_codes", align_bytes=64, offset=N)
+        nc.sync.dma_start(w2_codes[:], w2_words[0].rearrange("p c i -> p (c i)").bitcast(I32))
+        nc.gpsimd.memset(w2_plane[:].bitcast(I32), 0)
+        for q in range(4):
+            nc.sync.dma_start(
+                w2_plane[32 * q : 32 * q + 4, :].bitcast(I32),
+                w2_scales[0, 4 * q : 4 * q + 4, :].bitcast(I32),
+            )
+
+        w1_bf = [held.tile([P, PACK * H], BF16, name=f"w1_bf{a}", tag=f"stage{a}", align_bytes=64) for a in range(2)]
+        w1_codes = [held.tile([P, H], U32, name=f"w1_codes{a}", align_bytes=64) for a in range(2)]
+        w1_plane = [held.tile([P, H], U8, name=f"w1_plane{a}", align_bytes=64) for a in range(2)]
+        picked = {}
+        acc = {}
+
+        def cast_w1(copy, a, m0, m1):
+            dst = w1_bf[a][:].rearrange("p (t m j) -> p m j t", t=PACK, j=PACK)
+            src = w1_raw[a][:].rearrange("p j (m t) -> p m j t", t=PACK)
+            copy(dst[:, m0:m1], src[:, m0:m1])
+
+        def quantize_w1(a):
+            nc.vector.quantize_mx(w1_codes[a][:].bitcast(E4M3), w1_plane[a][:], w1_bf[a][:])
+
+        def gather_words(a, k):
+            tag = "tab1" if (a, k) == (0, 1) else f"picked{a}_{k}"
+            picked[a, k] = held.tile([P, BLOCK], U32, name=f"picked{a}_{k}", tag=tag, align_bytes=64)
+            window = tab[a][:].bitcast(U32)
+            nc.vector.tensor_copy(picked[a, k][:], window.indirect(offsets[:, 32 * k : 32 * (k + 1)]))
+
+        def first_product(a, k, slices):
+            for t in slices:
+                if a == 0:
+                    acc[k, t] = psum.tile([P, BLOCK], F32, name=f"acc{k}_{t}", tag=f"bank{t}")
+                cols = slice(P * t, P * (t + 1))
+                nc.tensor.matmul_mx(
+                    acc[k, t][:],
+                    lhsT=w1_codes[a][:, cols].bitcast(E4M3),
+                    lhsT_scale=w1_plane[a][:, cols],
+                    rhs=picked[a, k][:].bitcast(E5M2),
+                    rhs_scale=picked_scales[a][:, BLOCK * k : BLOCK * (k + 1)],
+                    start=(a == 0),
+                    stop=(a == 1),
+                )
+
+        cast_w1(nc.scalar.copy, 0, 0, P)
+        gather_words(0, 0)
+        quantize_w1(0)
+        first_product(0, 0, range(4))
+        cast_w1(nc.scalar.copy, 1, 0, 64)
+        cast_w1(nc.vector.tensor_copy, 1, 64, P)
+        quantize_w1(1)
+        turned = psum.tile([P, P], F32, name="turned", tag="bank7")
+        nc.tensor.transpose(turned[:], rows_sb[:], ident[:])
+        cols_sb = held.tile([P, 2 * N_TILES], F32, name="cols_sb")
+        nc.scalar.copy(cols_sb[:], turned[:, 0 : 2 * N_TILES])
+        gather_words(1, 0)
+        first_product(1, 0, range(4))
+        gather_words(1, 1)
+        gather_words(0, 1)
+
+        h_codes = {}
+        seen = {}
+        h_plane = {}
+
+        def code_chunk(c):
+            j0, width = CHUNKS[c]
+            k, lo = divmod(j0, BLOCK)
+            bounded = held.tile([P, PACK, width], F32, name=f"bounded{c}")
+            seen[("b", c)] = bounded
+            for t in range(PACK):
+                nc.scalar.activation(bounded[:, t, :], acc[k, t][:, lo : lo + width], ACT.Tanh, bias=b1_sb[:, t : t + 1])
+            h_bf = held.tile([P, PACK * width], BF16, name=f"h_bf{c}", tag="h_bf", align_bytes=64)
+            nc.vector.tensor_tensor(
+                h_bf[:].rearrange("p (c i t) -> p c t i", i=4, t=PACK),
+                bounded[:].rearrange("p t (c i) -> p c t i", i=4),
+                gain_sb[:].unsqueeze(1).unsqueeze(3).to_broadcast([P, width // 4, PACK, 4]),
+                ALU.mult,
+            )
+            h_codes[c] = held.tile([P, width], U32, name=f"h_codes{c}", align_bytes=64)
+            h_plane[c] = held.tile([P, width], U8, name=f"h_plane{c}", align_bytes=64)
+            nc.vector.quantize_mx(h_codes[c][:].bitcast(E4M3), h_plane[c][:], h_bf[:])
+
+        def expand_chunk(c, banks, on_scalar):
+            j0, width = CHUNKS[c]
+            per_bank = min(2, BLOCK // width)
+            for g in range(N_TILES // per_bank):
+                y = psum.tile([P, per_bank, width], F32, name=f"y{c}_{g}", tag=f"bank{banks[g % len(banks)]}")
+                for u in range(per_bank):
+                    cols = slice(P * (per_bank * g + u), P * (per_bank * g + u + 1))
+                    nc.tensor.matmul_mx(
+                        y[:, u, :],
+                        lhsT=w2_codes[:, cols].bitcast(E4M3),
+                        lhsT_scale=w2_plane[:, cols],
+                        rhs=h_codes[c][:].bitcast(E4M3),
+                        rhs_scale=h_plane[c][:],
+                        start=True,
+                        stop=True,
+                    )
+                result = held.tile([P, per_bank, width], F32, name=f"result{c}_{g}")
+                seen[("r", c, g)] = result
+                for u in range(per_bank):
+                    b = per_bank * g + u
+                    step_col = cols_sb[:, b : b + 1]
+                    drift_col = cols_sb[:, N_TILES + b : N_TILES + b + 1]
+                    if g in on_scalar:
+                        nc.scalar.activation(result[:, u, :], y[:, u, :], ACT.Identity, bias=drift_col, scale=step_col)
+                    else:
+                        nc.vector.tensor_scalar(result[:, u, :], y[:, u, :], step_col, drift_col, ALU.mult, ALU.add)
+                rows = out[P * per_bank * g : P * per_bank * (g + 1), j0 : j0 + width]
+                nc.sync.dma_start(rows.rearrange("(u p) j -> p u j", p=P), result[:])
+
+        code_chunk(0)
+        code_chunk(1)
+        expand_chunk(0, (4, 5, 6, 7), (0, 1, 2))
+        for t in range(PACK):
+            first_product(0, 1, (t,))
+            first_product(1, 1, (t,))
+        code_chunk(2)
+        expand_chunk(1, (4, 5, 6, 7), (0, 1, 2))
+        code_chunk(3)
+        expand_chunk(2, (4, 5, 6, 7), (0, 2))
+        expand_chunk(3, (0, 1, 2, 3), (0, 2))

@@ -21,8 +21,9 @@ P = 128
 PACK = 4
 K_PASS = P * PACK
 BLOCK = 512
-CHUNKS = [(0, 256), (256, 256), (512, 256), (768, 256)]
+HALF = 256
 N_TILES = N // P
+CAST_SPLIT = 64
 
 
 def tile_list_federated_client_updates_kernel(
@@ -31,14 +32,10 @@ def tile_list_federated_client_updates_kernel(
     nc = tc.nc
     with ExitStack() as ctx:
         held = ctx.enter_context(tc.tile_pool(name="held", bufs=1))
-        shared = ctx.enter_context(tc.tile_pool(name="shared", bufs=1))
         psum = ctx.enter_context(tc.psum_pool(name="psum", bufs=1))
 
         offsets = held.tile([P, S // 16], U16, name="offsets")
         nc.sync.dma_start(offsets[:], offs)
-
-        b1_sb = held.tile([P, PACK], F32, name="b1_sb")
-        gain_sb = held.tile([P, PACK], F32, name="gain_sb")
 
         w1_raw = [held.tile([P, PACK, H], F32, name=f"w1_raw{a}") for a in range(2)]
         tab = [held.tile([P, T], I32, name=f"tab{a}", tag=f"tab{a}", align_bytes=64) for a in range(2)]
@@ -51,42 +48,45 @@ def tile_list_federated_client_updates_kernel(
             nc.sync.dma_start(tab[a][:], tab_words[a].rearrange("p t i -> p (t i)").bitcast(I32))
 
         load_w1(0)
-        scale_window = shared.tile([P, T], U8, name="scale_window", align_bytes=64, offset=0)
+        scale_window = held.tile([P, T], U8, name="scale_window", tag="window", align_bytes=64)
         nc.gpsimd.memset(scale_window[:].bitcast(I32), 0)
         for q in range(4):
             nc.sync.dma_start(
                 scale_window[32 * q : 32 * q + 8, :].bitcast(I32),
                 tab_scales[:, 4 * q : 4 * q + 4, :].bitcast(I32),
             )
-        rows_sb = held.tile([P, P], F32, name="rows_sb")
-        ident = held.tile([P, P], F32, name="ident")
-        nc.gpsimd.memset(rows_sb[:], 0.0)
         load_table(0)
         load_w1(1)
         load_table(1)
-        nc.sync.dma_start(rows_sb[0:N_TILES, :], step.rearrange("(b p) -> b p", p=P))
-        nc.sync.dma_start(rows_sb[N_TILES : 2 * N_TILES, :], drift.rearrange("(b p) -> b p", p=P))
-        nc.sync.dma_start(b1_sb[:], b1.rearrange("(p t) -> p t", t=PACK))
-        nc.sync.dma_start(gain_sb[:], gain.rearrange("(p t) -> p t", t=PACK))
 
-        make_identity(nc, ident[:])
-
-        picked_scales = [held.tile([P, S], U8, name=f"picked_scales{a}", align_bytes=64) for a in range(2)]
-        nc.gpsimd.memset(picked_scales[1][:].bitcast(I32), 0)
-        nc.vector.tensor_copy(picked_scales[0][:], scale_window[:].indirect(offsets[:]))
-        nc.sync.dma_start(picked_scales[1][0:100, :].bitcast(I32), picked_scales[0][4:104, :].bitcast(I32))
-
-        w2_plane = shared.tile([P, N], U8, name="w2_plane", align_bytes=64, offset=0)
-        w2_codes = shared.tile([P, N], I32, name="w2_codes", align_bytes=64, offset=N)
-        nc.sync.dma_start(w2_codes[:], w2_words[0].rearrange("p c i -> p (c i)").bitcast(I32))
-        nc.gpsimd.memset(w2_plane[:].bitcast(I32), 0)
+        w2_plane = held.tile([P, N], U8, name="w2_plane", align_bytes=64)
+        nc.vector.memset(w2_plane[:].bitcast(I32), 0)
         for q in range(4):
             nc.sync.dma_start(
                 w2_plane[32 * q : 32 * q + 4, :].bitcast(I32),
                 w2_scales[0, 4 * q : 4 * q + 4, :].bitcast(I32),
             )
 
-        w1_bf = [held.tile([P, PACK * H], BF16, name=f"w1_bf{a}", tag=f"stage{a}", align_bytes=64) for a in range(2)]
+        ident = held.tile([P, P], F32, name="ident")
+        make_identity(nc, ident[:])
+        rows_sb = held.tile([P, P], F32, name="rows_sb")
+        nc.vector.memset(rows_sb[:], 0.0)
+        nc.gpsimd.dma_start(rows_sb[0:N_TILES, :], step.rearrange("(b p) -> b p", p=P))
+        nc.gpsimd.dma_start(rows_sb[N_TILES : 2 * N_TILES, :], drift.rearrange("(b p) -> b p", p=P))
+        b1_sb = held.tile([P, PACK], F32, name="b1_sb")
+        gain_sb = held.tile([P, PACK], F32, name="gain_sb")
+        nc.gpsimd.dma_start(b1_sb[:], b1.rearrange("(p t) -> p t", t=PACK))
+        nc.gpsimd.dma_start(gain_sb[:], gain.rearrange("(p t) -> p t", t=PACK))
+
+        picked_scales = [held.tile([P, S], U8, name=f"picked_scales{a}", align_bytes=64) for a in range(2)]
+        nc.vector.memset(picked_scales[1][:].bitcast(I32), 0)
+        nc.vector.tensor_copy(picked_scales[0][:], scale_window[:].indirect(offsets[:]))
+        nc.sync.dma_start(picked_scales[1][0:100, :].bitcast(I32), picked_scales[0][4:104, :].bitcast(I32))
+
+        w2_codes = held.tile([P, N], I32, name="w2_codes", tag="window", align_bytes=64)
+        nc.sync.dma_start(w2_codes[:], w2_words[0].rearrange("p c i -> p (c i)").bitcast(I32))
+
+        w1_bf = [held.tile([P, PACK * H], BF16, name=f"w1_bf{a}", align_bytes=64) for a in range(2)]
         w1_codes = [held.tile([P, H], U32, name=f"w1_codes{a}", align_bytes=64) for a in range(2)]
         w1_plane = [held.tile([P, H], U8, name=f"w1_plane{a}", align_bytes=64) for a in range(2)]
         picked = {}
@@ -100,16 +100,15 @@ def tile_list_federated_client_updates_kernel(
         def quantize_w1(a):
             nc.vector.quantize_mx(w1_codes[a][:].bitcast(E4M3), w1_plane[a][:], w1_bf[a][:])
 
-        def gather_words(a, k):
-            tag = "tab1" if (a, k) == (0, 1) else f"picked{a}_{k}"
+        def gather_words(a, k, tag):
             picked[a, k] = held.tile([P, BLOCK], U32, name=f"picked{a}_{k}", tag=tag, align_bytes=64)
             window = tab[a][:].bitcast(U32)
             nc.vector.tensor_copy(picked[a, k][:], window.indirect(offsets[:, 32 * k : 32 * (k + 1)]))
 
-        def first_product(a, k, slices):
-            for t in slices:
-                if a == 0:
-                    acc[k, t] = psum.tile([P, BLOCK], F32, name=f"acc{k}_{t}", tag=f"bank{t}")
+        def first_product(a, k, opens):
+            for t in range(PACK):
+                if opens:
+                    acc[k, t] = psum.tile([P, BLOCK], F32, name=f"acc{k}_{t}", tag=f"bank{PACK * k + t}")
                 cols = slice(P * t, P * (t + 1))
                 nc.tensor.matmul_mx(
                     acc[k, t][:],
@@ -117,85 +116,85 @@ def tile_list_federated_client_updates_kernel(
                     lhsT_scale=w1_plane[a][:, cols],
                     rhs=picked[a, k][:].bitcast(E5M2),
                     rhs_scale=picked_scales[a][:, BLOCK * k : BLOCK * (k + 1)],
-                    start=(a == 0),
-                    stop=(a == 1),
+                    start=opens,
+                    stop=not opens,
                 )
 
         cast_w1(nc.scalar.copy, 0, 0, P)
-        gather_words(0, 0)
+        gather_words(0, 0, "picked0_0")
         quantize_w1(0)
-        first_product(0, 0, range(4))
-        cast_w1(nc.scalar.copy, 1, 0, 64)
-        cast_w1(nc.vector.tensor_copy, 1, 64, P)
+        first_product(0, 0, True)
+        cast_w1(nc.scalar.copy, 1, 0, CAST_SPLIT)
+        cast_w1(nc.vector.tensor_copy, 1, CAST_SPLIT, P)
         quantize_w1(1)
         turned = psum.tile([P, P], F32, name="turned", tag="bank7")
         nc.tensor.transpose(turned[:], rows_sb[:], ident[:])
         cols_sb = held.tile([P, 2 * N_TILES], F32, name="cols_sb")
         nc.scalar.copy(cols_sb[:], turned[:, 0 : 2 * N_TILES])
-        gather_words(1, 0)
-        first_product(1, 0, range(4))
-        gather_words(1, 1)
-        gather_words(0, 1)
+        gather_words(1, 0, "picked1_0")
+        first_product(1, 0, False)
+        gather_words(1, 1, "picked1_1")
+        first_product(1, 1, True)
+        gather_words(0, 1, "tab1")
+        first_product(0, 1, False)
 
-        h_codes = {}
+        h_codes = [held.tile([P, BLOCK], U32, name=f"h_codes{k}", align_bytes=64) for k in range(2)]
+        h_plane = [held.tile([P, BLOCK], U8, name=f"h_plane{k}", align_bytes=64) for k in range(2)]
         seen = {}
-        h_plane = {}
 
-        def code_chunk(c):
-            j0, width = CHUNKS[c]
+        def code_columns(j0, width):
             k, lo = divmod(j0, BLOCK)
-            bounded = held.tile([P, PACK, width], F32, name=f"bounded{c}")
-            seen[("b", c)] = bounded
+            cols = slice(lo, lo + width)
+            bounded = held.tile([P, PACK, width], F32, name=f"bounded{j0}")
+            seen["b", j0] = bounded
             for t in range(PACK):
-                nc.scalar.activation(bounded[:, t, :], acc[k, t][:, lo : lo + width], ACT.Tanh, bias=b1_sb[:, t : t + 1])
-            h_bf = held.tile([P, PACK * width], BF16, name=f"h_bf{c}", tag="h_bf", align_bytes=64)
+                nc.scalar.activation(bounded[:, t, :], acc[k, t][:, cols], ACT.Tanh, bias=b1_sb[:, t : t + 1])
+            h_bf = held.tile([P, PACK * width], BF16, name=f"h_bf{j0}", tag="h_bf", align_bytes=64)
             nc.vector.tensor_tensor(
                 h_bf[:].rearrange("p (c i t) -> p c t i", i=4, t=PACK),
                 bounded[:].rearrange("p t (c i) -> p c t i", i=4),
                 gain_sb[:].unsqueeze(1).unsqueeze(3).to_broadcast([P, width // 4, PACK, 4]),
                 ALU.mult,
             )
-            h_codes[c] = held.tile([P, width], U32, name=f"h_codes{c}", align_bytes=64)
-            h_plane[c] = held.tile([P, width], U8, name=f"h_plane{c}", align_bytes=64)
-            nc.vector.quantize_mx(h_codes[c][:].bitcast(E4M3), h_plane[c][:], h_bf[:])
+            nc.vector.quantize_mx(h_codes[k][:, cols].bitcast(E4M3), h_plane[k][:, cols], h_bf[:])
 
-        def expand_chunk(c, banks, on_scalar):
-            j0, width = CHUNKS[c]
-            per_bank = min(2, BLOCK // width)
-            for g in range(N_TILES // per_bank):
-                y = psum.tile([P, per_bank, width], F32, name=f"y{c}_{g}", tag=f"bank{banks[g % len(banks)]}")
-                for u in range(per_bank):
-                    cols = slice(P * (per_bank * g + u), P * (per_bank * g + u + 1))
-                    nc.tensor.matmul_mx(
-                        y[:, u, :],
-                        lhsT=w2_codes[:, cols].bitcast(E4M3),
-                        lhsT_scale=w2_plane[:, cols],
-                        rhs=h_codes[c][:].bitcast(E4M3),
-                        rhs_scale=h_plane[c][:],
-                        start=True,
-                        stop=True,
-                    )
-                result = held.tile([P, per_bank, width], F32, name=f"result{c}_{g}")
-                seen[("r", c, g)] = result
-                for u in range(per_bank):
-                    b = per_bank * g + u
-                    step_col = cols_sb[:, b : b + 1]
-                    drift_col = cols_sb[:, N_TILES + b : N_TILES + b + 1]
-                    if g in on_scalar:
-                        nc.scalar.activation(result[:, u, :], y[:, u, :], ACT.Identity, bias=drift_col, scale=step_col)
-                    else:
-                        nc.vector.tensor_scalar(result[:, u, :], y[:, u, :], step_col, drift_col, ALU.mult, ALU.add)
-                rows = out[P * per_bank * g : P * per_bank * (g + 1), j0 : j0 + width]
-                nc.sync.dma_start(rows.rearrange("(u p) j -> p u j", p=P), result[:])
+        def expand(b0, j0, width, bank, on_scalar):
+            k, lo = divmod(j0, BLOCK)
+            moving = slice(lo, lo + width)
+            count = BLOCK // width
+            y = psum.tile([P, count, width], F32, name=f"y{b0}_{j0}", tag=f"bank{bank}")
+            for u in range(count):
+                cols = slice(P * (b0 + u), P * (b0 + u + 1))
+                nc.tensor.matmul_mx(
+                    y[:, u, :],
+                    lhsT=w2_codes[:, cols].bitcast(E4M3),
+                    lhsT_scale=w2_plane[:, cols],
+                    rhs=h_codes[k][:, moving].bitcast(E4M3),
+                    rhs_scale=h_plane[k][:, moving],
+                    start=True,
+                    stop=True,
+                )
+            result = held.tile([P, count, width], F32, name=f"result{b0}_{j0}")
+            seen["r", b0, j0] = result
+            for u in range(count):
+                b = b0 + u
+                step_col = cols_sb[:, b : b + 1]
+                drift_col = cols_sb[:, N_TILES + b : N_TILES + b + 1]
+                if on_scalar:
+                    nc.scalar.activation(result[:, u, :], y[:, u, :], ACT.Identity, bias=drift_col, scale=step_col)
+                else:
+                    nc.vector.tensor_scalar(result[:, u, :], y[:, u, :], step_col, drift_col, ALU.mult, ALU.add)
+            rows = out[P * b0 : P * (b0 + count), j0 : j0 + width]
+            nc.sync.dma_start(rows.rearrange("(u p) j -> p u j", p=P), result[:])
 
-        code_chunk(0)
-        code_chunk(1)
-        expand_chunk(0, (4, 5, 6, 7), (0, 1, 2))
-        for t in range(PACK):
-            first_product(0, 1, (t,))
-            first_product(1, 1, (t,))
-        code_chunk(2)
-        expand_chunk(1, (4, 5, 6, 7), (0, 1, 2))
-        code_chunk(3)
-        expand_chunk(2, (4, 5, 6, 7), (0, 2))
-        expand_chunk(3, (0, 1, 2, 3), (0, 2))
+        code_columns(0, HALF)
+        code_columns(HALF, HALF)
+        expand(0, 0, HALF, 0, True)
+        expand(2, 0, HALF, 1, False)
+        code_columns(BLOCK, BLOCK)
+        for b in range(4, 8):
+            expand(b, 0, BLOCK, (b - 2) % 4, True)
+        expand(0, HALF, HALF, 2, False)
+        expand(2, HALF, HALF, 3, True)
+        for b in range(N_TILES):
+            expand(b, BLOCK, BLOCK, (b + 4) % 8, b % 2 == 1)

@@ -21,9 +21,12 @@ P = 128
 PACK = 4
 K_PASS = P * PACK
 BLOCK = 512
-HALF = 256
 N_TILES = N // P
-CAST_SPLIT = 64
+CAST_SCALAR = (64, 84, 46)
+CHUNK = 256
+PAIR = 2
+PAIR_BYTES = PAIR * H * 4
+WINDOW_OFFSET = PAIR_BYTES - 512
 
 
 def tile_list_federated_client_updates_kernel(
@@ -32,34 +35,118 @@ def tile_list_federated_client_updates_kernel(
     nc = tc.nc
     with ExitStack() as ctx:
         held = ctx.enter_context(tc.tile_pool(name="held", bufs=1))
+        shared = ctx.enter_context(tc.tile_pool(name="shared", bufs=1))
         psum = ctx.enter_context(tc.psum_pool(name="psum", bufs=1))
 
         offsets = held.tile([P, S // 16], U16, name="offsets")
         nc.sync.dma_start(offsets[:], offs)
 
-        w1_raw = [held.tile([P, PACK, H], F32, name=f"w1_raw{a}") for a in range(2)]
+        w1_first = held.tile([P, PACK, H], F32, name="w1_first", tag="w1_first", align_bytes=64)
+        w1_last = [
+            shared.tile([P, PAIR, H], F32, name=f"w1_last{u}", offset=u * (PAIR_BYTES + N), align_bytes=64)
+            for u in range(2)
+        ]
         tab = [held.tile([P, T], I32, name=f"tab{a}", tag=f"tab{a}", align_bytes=64) for a in range(2)]
 
-        def load_w1(a):
-            rows = w1[K_PASS * a : K_PASS * (a + 1), :]
-            nc.sync.dma_start(w1_raw[a][:], rows.rearrange("(p j) c -> p j c", j=PACK))
+        w1_rows = w1.rearrange("(a p j) c -> a p j c", p=P, j=PACK)
 
-        def load_table(a):
-            nc.sync.dma_start(tab[a][:], tab_words[a].rearrange("p t i -> p (t i)").bitcast(I32))
+        def load_table(a, t0, t1):
+            words = tab_words[a].rearrange("p t i -> p (t i)").bitcast(I32)
+            nc.sync.dma_start(tab[a][:, t0:t1], words[:, t0:t1])
 
-        load_w1(0)
-        scale_window = held.tile([P, T], U8, name="scale_window", tag="window", align_bytes=64)
+        load_table(0, 0, T // 2)
+        scale_window = shared.tile([P, T], U8, name="scale_window", offset=WINDOW_OFFSET, align_bytes=64)
         nc.gpsimd.memset(scale_window[:].bitcast(I32), 0)
-        for q in range(4):
-            nc.sync.dma_start(
-                scale_window[32 * q : 32 * q + 8, :].bitcast(I32),
-                tab_scales[:, 4 * q : 4 * q + 4, :].bitcast(I32),
-            )
-        load_table(0)
-        load_w1(1)
-        load_table(1)
+        scale_rows = tab_scales.rearrange("a q t -> (a q) t").bitcast(I32)
+        nc.sync.dma_start(scale_window[0:P:4, :].bitcast(I32), scale_rows)
+        load_table(0, T // 2, T)
+        nc.sync.dma_start(w1_first[:], w1_rows[0])
+        rows_sb = held.tile([P, P], F32, name="rows_sb")
+        nc.vector.memset(rows_sb[:], 0.0)
+        nc.sync.dma_start(rows_sb[0:N_TILES, :], step.rearrange("(b p) -> b p", p=P))
+        nc.sync.dma_start(rows_sb[N_TILES : 2 * N_TILES, :], drift.rearrange("(b p) -> b p", p=P))
+        load_table(1, 0, T)
 
-        w2_plane = held.tile([P, N], U8, name="w2_plane", align_bytes=64)
+        ident = held.tile([P, P], F32, name="ident")
+        make_identity(nc, ident[:])
+        b1_sb = held.tile([P, PACK], F32, name="b1_sb")
+        gain_sb = held.tile([P, PACK], F32, name="gain_sb")
+        nc.gpsimd.dma_start(b1_sb[:], b1.rearrange("(p t) -> p t", t=PACK))
+        nc.gpsimd.dma_start(gain_sb[:], gain.rearrange("(p t) -> p t", t=PACK))
+
+        picked_rows = held.tile([P, S], U8, name="picked_rows", align_bytes=64)
+        picked_scales = [held.tile([P, S], U8, name=f"picked_scales{a}", align_bytes=64) for a in range(2)]
+        for a in range(2):
+            nc.vector.memset(picked_scales[a][:].bitcast(I32), 0)
+        nc.vector.tensor_copy(picked_rows[:], scale_window[:].indirect(offsets[:]))
+
+        def move_scale_rows(a):
+            for q in range(4):
+                first = 64 * a + 16 * q
+                nc.sync.dma_start(
+                    picked_scales[a][32 * q : 32 * q + 4, :].bitcast(I32),
+                    picked_rows[first : first + 16 : 4, :].bitcast(I32),
+                )
+
+        move_scale_rows(0)
+        for u in range(2):
+            nc.sync.dma_start(w1_last[u][:], w1_rows[1][:, PAIR * u : PAIR * (u + 1), :])
+        move_scale_rows(1)
+
+        turned = psum.tile([P, P], F32, name="turned", tag="bank7")
+        nc.tensor.transpose(turned[:], rows_sb[:], ident[:])
+        cols_sb = held.tile([P, 2 * N_TILES], F32, name="cols_sb")
+        nc.scalar.copy(cols_sb[:], turned[:, 0 : 2 * N_TILES])
+
+        w1_bf = [held.tile([P, PACK * H], BF16, name=f"w1_bf{a}", tag=f"w1_bf{a}", align_bytes=64) for a in range(2)]
+        w1_codes = [held.tile([P, H], U32, name=f"w1_codes{a}", align_bytes=64) for a in range(2)]
+        w1_plane = [held.tile([P, H], U8, name=f"w1_plane{a}", align_bytes=64) for a in range(2)]
+        picked = {}
+        acc = {}
+
+        def cast_w1(a, raw, j0, j1, split):
+            dst = w1_bf[a][:].rearrange("p (t m j) -> p m j t", t=PACK, j=PACK)[:, :, j0:j1]
+            src = raw[:].rearrange("p j (m t) -> p m j t", t=PACK)
+            nc.scalar.copy(dst[:, 0:split], src[:, 0:split])
+            nc.vector.tensor_copy(dst[:, split:P], src[:, split:P])
+
+        def quantize_w1(a, c0, c1):
+            nc.vector.quantize_mx(
+                w1_codes[a][:, c0:c1].bitcast(E4M3), w1_plane[a][:, c0:c1], w1_bf[a][:, PACK * c0 : PACK * c1]
+            )
+
+        def gather_words(a, k, tag):
+            picked[a, k] = held.tile([P, BLOCK], U32, name=f"picked{a}_{k}", tag=tag, align_bytes=64)
+            window = tab[a][:].bitcast(U32)
+            nc.vector.tensor_copy(picked[a, k][:], window.indirect(offsets[:, 32 * k : 32 * (k + 1)]))
+
+        def first_product(a, k, t, bank):
+            if a == 0:
+                acc[k, t] = psum.tile([P, BLOCK], F32, name=f"acc{k}_{t}", tag=f"bank{bank}")
+            cols = slice(P * t, P * (t + 1))
+            nc.tensor.matmul_mx(
+                acc[k, t][:],
+                lhsT=w1_codes[a][:, cols].bitcast(E4M3),
+                lhsT_scale=w1_plane[a][:, cols],
+                rhs=picked[a, k][:].bitcast(E5M2),
+                rhs_scale=picked_scales[a][:, BLOCK * k : BLOCK * (k + 1)],
+                start=a == 0,
+                stop=a == 1,
+            )
+
+        gather_words(0, 0, "picked0_0")
+        cast_w1(0, w1_first, 0, PACK, CAST_SCALAR[0])
+        quantize_w1(0, 0, H)
+        for t in range(PACK):
+            first_product(0, 0, t, t)
+        gather_words(0, 1, "w1_bf0")
+        for t in range(PACK - 1):
+            first_product(0, 1, t, PACK + t)
+        gather_words(1, 0, "picked1_0")
+
+        w2_codes = held.tile([P, N], I32, name="w2_codes", tag="w1_first", align_bytes=64)
+        nc.sync.dma_start(w2_codes[:], w2_words[0].rearrange("p c i -> p (c i)").bitcast(I32))
+        w2_plane = shared.tile([P, N], U8, name="w2_plane", offset=PAIR_BYTES, align_bytes=64)
         nc.vector.memset(w2_plane[:].bitcast(I32), 0)
         for q in range(4):
             nc.sync.dma_start(
@@ -67,88 +154,26 @@ def tile_list_federated_client_updates_kernel(
                 w2_scales[0, 4 * q : 4 * q + 4, :].bitcast(I32),
             )
 
-        ident = held.tile([P, P], F32, name="ident")
-        make_identity(nc, ident[:])
-        rows_sb = held.tile([P, P], F32, name="rows_sb")
-        nc.vector.memset(rows_sb[:], 0.0)
-        nc.gpsimd.dma_start(rows_sb[0:N_TILES, :], step.rearrange("(b p) -> b p", p=P))
-        nc.gpsimd.dma_start(rows_sb[N_TILES : 2 * N_TILES, :], drift.rearrange("(b p) -> b p", p=P))
-        b1_sb = held.tile([P, PACK], F32, name="b1_sb")
-        gain_sb = held.tile([P, PACK], F32, name="gain_sb")
-        nc.gpsimd.dma_start(b1_sb[:], b1.rearrange("(p t) -> p t", t=PACK))
-        nc.gpsimd.dma_start(gain_sb[:], gain.rearrange("(p t) -> p t", t=PACK))
+        for u in range(2):
+            cast_w1(1, w1_last[u], PAIR * u, PAIR * (u + 1), CAST_SCALAR[1 + u])
+        for t in range(PACK):
+            quantize_w1(1, P * t, P * (t + 1))
+        for t in range(PACK):
+            first_product(1, 0, t, t)
+        gather_words(1, 1, "w1_bf1")
+        for t in range(PACK - 1):
+            first_product(1, 1, t, PACK + t)
 
-        picked_scales = [held.tile([P, S], U8, name=f"picked_scales{a}", align_bytes=64) for a in range(2)]
-        nc.vector.memset(picked_scales[1][:].bitcast(I32), 0)
-        nc.vector.tensor_copy(picked_scales[0][:], scale_window[:].indirect(offsets[:]))
-        nc.sync.dma_start(picked_scales[1][0:100, :].bitcast(I32), picked_scales[0][4:104, :].bitcast(I32))
-
-        w2_codes = held.tile([P, N], I32, name="w2_codes", tag="window", align_bytes=64)
-        nc.sync.dma_start(w2_codes[:], w2_words[0].rearrange("p c i -> p (c i)").bitcast(I32))
-
-        w1_bf = [held.tile([P, PACK * H], BF16, name=f"w1_bf{a}", align_bytes=64) for a in range(2)]
-        w1_codes = [held.tile([P, H], U32, name=f"w1_codes{a}", align_bytes=64) for a in range(2)]
-        w1_plane = [held.tile([P, H], U8, name=f"w1_plane{a}", align_bytes=64) for a in range(2)]
-        picked = {}
-        acc = {}
-
-        def cast_w1(copy, a, m0, m1):
-            dst = w1_bf[a][:].rearrange("p (t m j) -> p m j t", t=PACK, j=PACK)
-            src = w1_raw[a][:].rearrange("p j (m t) -> p m j t", t=PACK)
-            copy(dst[:, m0:m1], src[:, m0:m1])
-
-        def quantize_w1(a):
-            nc.vector.quantize_mx(w1_codes[a][:].bitcast(E4M3), w1_plane[a][:], w1_bf[a][:])
-
-        def gather_words(a, k, tag):
-            picked[a, k] = held.tile([P, BLOCK], U32, name=f"picked{a}_{k}", tag=tag, align_bytes=64)
-            window = tab[a][:].bitcast(U32)
-            nc.vector.tensor_copy(picked[a, k][:], window.indirect(offsets[:, 32 * k : 32 * (k + 1)]))
-
-        def first_product(a, k, opens):
-            for t in range(PACK):
-                if opens:
-                    acc[k, t] = psum.tile([P, BLOCK], F32, name=f"acc{k}_{t}", tag=f"bank{PACK * k + t}")
-                cols = slice(P * t, P * (t + 1))
-                nc.tensor.matmul_mx(
-                    acc[k, t][:],
-                    lhsT=w1_codes[a][:, cols].bitcast(E4M3),
-                    lhsT_scale=w1_plane[a][:, cols],
-                    rhs=picked[a, k][:].bitcast(E5M2),
-                    rhs_scale=picked_scales[a][:, BLOCK * k : BLOCK * (k + 1)],
-                    start=opens,
-                    stop=not opens,
-                )
-
-        cast_w1(nc.scalar.copy, 0, 0, P)
-        gather_words(0, 0, "picked0_0")
-        quantize_w1(0)
-        first_product(0, 0, True)
-        cast_w1(nc.scalar.copy, 1, 0, CAST_SPLIT)
-        cast_w1(nc.vector.tensor_copy, 1, CAST_SPLIT, P)
-        quantize_w1(1)
-        turned = psum.tile([P, P], F32, name="turned", tag="bank7")
-        nc.tensor.transpose(turned[:], rows_sb[:], ident[:])
-        cols_sb = held.tile([P, 2 * N_TILES], F32, name="cols_sb")
-        nc.scalar.copy(cols_sb[:], turned[:, 0 : 2 * N_TILES])
-        gather_words(1, 0, "picked1_0")
-        first_product(1, 0, False)
-        gather_words(1, 1, "picked1_1")
-        first_product(1, 1, True)
-        gather_words(0, 1, "tab1")
-        first_product(0, 1, False)
-
-        h_codes = [held.tile([P, BLOCK], U32, name=f"h_codes{k}", align_bytes=64) for k in range(2)]
-        h_plane = [held.tile([P, BLOCK], U8, name=f"h_plane{k}", align_bytes=64) for k in range(2)]
-        seen = {}
+        h_codes = held.tile([P, S], U32, name="h_codes", align_bytes=64)
+        h_plane = held.tile([P, S], U8, name="h_plane", align_bytes=64)
 
         def code_columns(j0, width):
             k, lo = divmod(j0, BLOCK)
-            cols = slice(lo, lo + width)
             bounded = held.tile([P, PACK, width], F32, name=f"bounded{j0}")
-            seen["b", j0] = bounded
             for t in range(PACK):
-                nc.scalar.activation(bounded[:, t, :], acc[k, t][:, cols], ACT.Tanh, bias=b1_sb[:, t : t + 1])
+                nc.scalar.activation(
+                    bounded[:, t, :], acc[k, t][:, lo : lo + width], ACT.Tanh, bias=b1_sb[:, t : t + 1]
+                )
             h_bf = held.tile([P, PACK * width], BF16, name=f"h_bf{j0}", tag="h_bf", align_bytes=64)
             nc.vector.tensor_tensor(
                 h_bf[:].rearrange("p (c i t) -> p c t i", i=4, t=PACK),
@@ -156,11 +181,11 @@ def tile_list_federated_client_updates_kernel(
                 gain_sb[:].unsqueeze(1).unsqueeze(3).to_broadcast([P, width // 4, PACK, 4]),
                 ALU.mult,
             )
-            nc.vector.quantize_mx(h_codes[k][:, cols].bitcast(E4M3), h_plane[k][:, cols], h_bf[:])
+            cols = slice(j0, j0 + width)
+            nc.vector.quantize_mx(h_codes[:, cols].bitcast(E4M3), h_plane[:, cols], h_bf[:])
 
-        def expand(b0, j0, width, bank, on_scalar):
-            k, lo = divmod(j0, BLOCK)
-            moving = slice(lo, lo + width)
+        def expand(b0, j0, width, bank, on_scalar, split=False):
+            moving = slice(j0, j0 + width)
             count = BLOCK // width
             y = psum.tile([P, count, width], F32, name=f"y{b0}_{j0}", tag=f"bank{bank}")
             for u in range(count):
@@ -169,13 +194,12 @@ def tile_list_federated_client_updates_kernel(
                     y[:, u, :],
                     lhsT=w2_codes[:, cols].bitcast(E4M3),
                     lhsT_scale=w2_plane[:, cols],
-                    rhs=h_codes[k][:, moving].bitcast(E4M3),
-                    rhs_scale=h_plane[k][:, moving],
+                    rhs=h_codes[:, moving].bitcast(E4M3),
+                    rhs_scale=h_plane[:, moving],
                     start=True,
                     stop=True,
                 )
             result = held.tile([P, count, width], F32, name=f"result{b0}_{j0}")
-            seen["r", b0, j0] = result
             for u in range(count):
                 b = b0 + u
                 step_col = cols_sb[:, b : b + 1]
@@ -184,17 +208,23 @@ def tile_list_federated_client_updates_kernel(
                     nc.scalar.activation(result[:, u, :], y[:, u, :], ACT.Identity, bias=drift_col, scale=step_col)
                 else:
                     nc.vector.tensor_scalar(result[:, u, :], y[:, u, :], step_col, drift_col, ALU.mult, ALU.add)
-            rows = out[P * b0 : P * (b0 + count), j0 : j0 + width]
-            nc.sync.dma_start(rows.rearrange("(u p) j -> p u j", p=P), result[:])
+            rows = out[P * b0 : P * (b0 + count), j0 : j0 + width].rearrange("(u p) j -> p u j", p=P)
+            if split:
+                for u in range(count):
+                    nc.sync.dma_start(rows[:, u, :], result[:, u, :])
+            else:
+                nc.sync.dma_start(rows, result[:])
 
-        code_columns(0, HALF)
-        code_columns(HALF, HALF)
-        expand(0, 0, HALF, 0, True)
-        expand(2, 0, HALF, 1, False)
+        code_columns(0, CHUNK)
+        code_columns(CHUNK, CHUNK)
+        expand(0, 0, CHUNK, 7, True, True)
+        for a in range(2):
+            first_product(a, 1, PACK - 1, 0)
+        expand(2, 0, CHUNK, 1, False)
         code_columns(BLOCK, BLOCK)
         for b in range(4, 8):
-            expand(b, 0, BLOCK, (b - 2) % 4, True)
-        expand(0, HALF, HALF, 2, False)
-        expand(2, HALF, HALF, 3, True)
+            expand(b, 0, BLOCK, (2, 3, 7, 1)[b - 4], True)
+        expand(0, CHUNK, CHUNK, 2, False)
+        expand(2, CHUNK, CHUNK, 3, True)
         for b in range(N_TILES):
             expand(b, BLOCK, BLOCK, (b + 4) % 8, b % 2 == 1)

@@ -22,7 +22,7 @@ PACK = 4
 K_PASS = P * PACK
 BLOCK = 512
 N_TILES = N // P
-CAST_SCALAR = (64, 84, 46)
+CAST_SCALAR = (52, 84, 46)
 CHUNK = 256
 PAIR = 2
 PAIR_BYTES = PAIR * H * 4
@@ -164,28 +164,35 @@ def tile_list_federated_client_updates_kernel(
         for t in range(PACK - 1):
             first_product(1, 1, t, PACK + t)
 
-        h_codes = held.tile([P, S], U32, name="h_codes", align_bytes=64)
         h_plane = held.tile([P, S], U8, name="h_plane", align_bytes=64)
+        bounded = {}
+        h_bf = {}
+        h_codes = [held.tile([P, BLOCK], U32, name=f"h_codes{k}", align_bytes=64) for k in range(2)]
 
-        def code_columns(j0, width):
+        def bound(j0, width):
             k, lo = divmod(j0, BLOCK)
-            bounded = held.tile([P, PACK, width], F32, name=f"bounded{j0}")
+            bounded[j0] = held.tile([P, PACK, width], F32, name=f"bounded{j0}")
+            h_bf[j0] = held.tile([P, PACK * width], BF16, name=f"h_bf{j0}", align_bytes=64)
             for t in range(PACK):
                 nc.scalar.activation(
-                    bounded[:, t, :], acc[k, t][:, lo : lo + width], ACT.Tanh, bias=b1_sb[:, t : t + 1]
+                    bounded[j0][:, t, :], acc[k, t][:, lo : lo + width], ACT.Tanh, bias=b1_sb[:, t : t + 1]
                 )
-            h_bf = held.tile([P, PACK * width], BF16, name=f"h_bf{j0}", tag="h_bf", align_bytes=64)
-            nc.vector.tensor_tensor(
-                h_bf[:].rearrange("p (c i t) -> p c t i", i=4, t=PACK),
-                bounded[:].rearrange("p t (c i) -> p c t i", i=4),
-                gain_sb[:].unsqueeze(1).unsqueeze(3).to_broadcast([P, width // 4, PACK, 4]),
-                ALU.mult,
-            )
-            cols = slice(j0, j0 + width)
-            nc.vector.quantize_mx(h_codes[:, cols].bitcast(E4M3), h_plane[:, cols], h_bf[:])
 
-        def expand(b0, j0, width, bank, on_scalar, split=False):
-            moving = slice(j0, j0 + width)
+        def weave(j0, c0, c1):
+            woven = h_bf[j0][:].rearrange("p (c i t) -> p c t i", i=4, t=PACK)
+            planes = bounded[j0][:].rearrange("p t (c i) -> p c t i", i=4)
+            groups = slice(c0 // 4, c1 // 4)
+            spread = gain_sb[:].unsqueeze(1).unsqueeze(3).to_broadcast([P, (c1 - c0) // 4, PACK, 4])
+            nc.vector.tensor_tensor(woven[:, groups], planes[:, groups], spread, ALU.mult)
+
+        def quantize_h(j0, width):
+            k, lo = divmod(j0, BLOCK)
+            nc.vector.quantize_mx(
+                h_codes[k][:, lo : lo + width].bitcast(E4M3), h_plane[:, j0 : j0 + width], h_bf[j0][:]
+            )
+
+        def multiply(b0, j0, width, bank):
+            k, lo = divmod(j0, BLOCK)
             count = BLOCK // width
             y = psum.tile([P, count, width], F32, name=f"y{b0}_{j0}", tag=f"bank{bank}")
             for u in range(count):
@@ -194,34 +201,51 @@ def tile_list_federated_client_updates_kernel(
                     y[:, u, :],
                     lhsT=w2_codes[:, cols].bitcast(E4M3),
                     lhsT_scale=w2_plane[:, cols],
-                    rhs=h_codes[:, moving].bitcast(E4M3),
-                    rhs_scale=h_plane[:, moving],
+                    rhs=h_codes[k][:, lo : lo + width].bitcast(E4M3),
+                    rhs_scale=h_plane[:, j0 : j0 + width],
                     start=True,
                     stop=True,
                 )
+            return y
+
+        def finish(result, y, b, on_scalar):
+            step_col = cols_sb[:, b : b + 1]
+            drift_col = cols_sb[:, N_TILES + b : N_TILES + b + 1]
+            if on_scalar:
+                nc.scalar.activation(result, y, ACT.Identity, bias=drift_col, scale=step_col)
+            else:
+                nc.vector.tensor_scalar(result, y, step_col, drift_col, ALU.mult, ALU.add)
+
+        def store_tile(y, u, b, j0, width, on_scalar):
+            result = held.tile([P, width], F32, name=f"single{b}_{j0}")
+            finish(result[:], y[:, u, :], b, on_scalar)
+            nc.sync.dma_start(out[P * b : P * (b + 1), j0 : j0 + width], result[:])
+
+        def expand(b0, j0, width, bank, on_scalar):
+            y = multiply(b0, j0, width, bank)
+            count = BLOCK // width
             result = held.tile([P, count, width], F32, name=f"result{b0}_{j0}")
             for u in range(count):
-                b = b0 + u
-                step_col = cols_sb[:, b : b + 1]
-                drift_col = cols_sb[:, N_TILES + b : N_TILES + b + 1]
-                if on_scalar:
-                    nc.scalar.activation(result[:, u, :], y[:, u, :], ACT.Identity, bias=drift_col, scale=step_col)
-                else:
-                    nc.vector.tensor_scalar(result[:, u, :], y[:, u, :], step_col, drift_col, ALU.mult, ALU.add)
+                finish(result[:, u, :], y[:, u, :], b0 + u, on_scalar)
             rows = out[P * b0 : P * (b0 + count), j0 : j0 + width].rearrange("(u p) j -> p u j", p=P)
-            if split:
-                for u in range(count):
-                    nc.sync.dma_start(rows[:, u, :], result[:, u, :])
-            else:
-                nc.sync.dma_start(rows, result[:])
+            nc.sync.dma_start(rows, result[:])
 
-        code_columns(0, CHUNK)
-        code_columns(CHUNK, CHUNK)
-        expand(0, 0, CHUNK, 7, True, True)
+        bound(0, CHUNK)
+        bound(CHUNK, CHUNK)
+        weave(0, 0, CHUNK)
+        weave(CHUNK, 0, CHUNK // 4)
+        quantize_h(0, CHUNK)
+        weave(CHUNK, CHUNK // 4, CHUNK)
+        first_y = multiply(0, 0, CHUNK, 7)
+        store_tile(first_y, 0, 0, 0, CHUNK, False)
+        quantize_h(CHUNK, CHUNK)
+        store_tile(first_y, 1, 1, 0, CHUNK, False)
         for a in range(2):
             first_product(a, 1, PACK - 1, 0)
-        expand(2, 0, CHUNK, 1, False)
-        code_columns(BLOCK, BLOCK)
+        bound(BLOCK, BLOCK)
+        expand(2, 0, CHUNK, 1, True)
+        weave(BLOCK, 0, BLOCK)
+        quantize_h(BLOCK, BLOCK)
         for b in range(4, 8):
             expand(b, 0, BLOCK, (2, 3, 7, 1)[b - 4], True)
         expand(0, CHUNK, CHUNK, 2, False)

@@ -22,8 +22,9 @@ PACK = 4
 K_PASS = P * PACK
 BLOCK = 512
 N_TILES = N // P
-CAST_SCALAR = (52, 84, 46)
+CAST_SCALAR = (60, 92, 48)
 CHUNK = 256
+COVER = 64
 PAIR = 2
 PAIR_BYTES = PAIR * H * 4
 WINDOW_OFFSET = PAIR_BYTES - 512
@@ -39,7 +40,6 @@ def tile_list_federated_client_updates_kernel(
         psum = ctx.enter_context(tc.psum_pool(name="psum", bufs=1))
 
         offsets = held.tile([P, S // 16], U16, name="offsets")
-        nc.sync.dma_start(offsets[:], offs)
 
         w1_first = held.tile([P, PACK, H], F32, name="w1_first", tag="w1_first", align_bytes=64)
         w1_last = [
@@ -55,6 +55,7 @@ def tile_list_federated_client_updates_kernel(
             nc.sync.dma_start(tab[a][:, t0:t1], words[:, t0:t1])
 
         load_table(0, 0, T // 2)
+        nc.sync.dma_start(offsets[:], offs)
         scale_window = shared.tile([P, T], U8, name="scale_window", offset=WINDOW_OFFSET, align_bytes=64)
         nc.gpsimd.memset(scale_window[:].bitcast(I32), 0)
         scale_rows = tab_scales.rearrange("a q t -> (a q) t").bitcast(I32)
@@ -115,8 +116,8 @@ def tile_list_federated_client_updates_kernel(
                 w1_codes[a][:, c0:c1].bitcast(E4M3), w1_plane[a][:, c0:c1], w1_bf[a][:, PACK * c0 : PACK * c1]
             )
 
-        def gather_words(a, k, tag):
-            picked[a, k] = held.tile([P, BLOCK], U32, name=f"picked{a}_{k}", tag=tag, align_bytes=64)
+        def gather_words(a, k, pool, **place):
+            picked[a, k] = pool.tile([P, BLOCK], U32, name=f"picked{a}_{k}", align_bytes=64, **place)
             window = tab[a][:].bitcast(U32)
             nc.vector.tensor_copy(picked[a, k][:], window.indirect(offsets[:, 32 * k : 32 * (k + 1)]))
 
@@ -134,15 +135,15 @@ def tile_list_federated_client_updates_kernel(
                 stop=a == 1,
             )
 
-        gather_words(0, 0, "picked0_0")
+        gather_words(0, 0, held)
         cast_w1(0, w1_first, 0, PACK, CAST_SCALAR[0])
         quantize_w1(0, 0, H)
         for t in range(PACK):
             first_product(0, 0, t, t)
-        gather_words(0, 1, "w1_bf0")
+        gather_words(0, 1, held, tag="w1_bf0")
         for t in range(PACK - 1):
             first_product(0, 1, t, PACK + t)
-        gather_words(1, 0, "picked1_0")
+        gather_words(1, 0, held)
 
         w2_codes = held.tile([P, N], I32, name="w2_codes", tag="w1_first", align_bytes=64)
         nc.sync.dma_start(w2_codes[:], w2_words[0].rearrange("p c i -> p (c i)").bitcast(I32))
@@ -160,7 +161,7 @@ def tile_list_federated_client_updates_kernel(
             quantize_w1(1, P * t, P * (t + 1))
         for t in range(PACK):
             first_product(1, 0, t, t)
-        gather_words(1, 1, "w1_bf1")
+        gather_words(1, 1, held, tag="w1_bf1")
         for t in range(PACK - 1):
             first_product(1, 1, t, PACK + t)
 
@@ -185,15 +186,16 @@ def tile_list_federated_client_updates_kernel(
             spread = gain_sb[:].unsqueeze(1).unsqueeze(3).to_broadcast([P, (c1 - c0) // 4, PACK, 4])
             nc.vector.tensor_tensor(woven[:, groups], planes[:, groups], spread, ALU.mult)
 
-        def quantize_h(j0, width):
+        def quantize_h(j0, c0, c1):
             k, lo = divmod(j0, BLOCK)
             nc.vector.quantize_mx(
-                h_codes[k][:, lo : lo + width].bitcast(E4M3), h_plane[:, j0 : j0 + width], h_bf[j0][:]
+                h_codes[k][:, lo + c0 : lo + c1].bitcast(E4M3),
+                h_plane[:, j0 + c0 : j0 + c1],
+                h_bf[j0][:, PACK * c0 : PACK * c1],
             )
 
-        def multiply(b0, j0, width, bank):
+        def multiply(b0, count, j0, width, bank):
             k, lo = divmod(j0, BLOCK)
-            count = BLOCK // width
             y = psum.tile([P, count, width], F32, name=f"y{b0}_{j0}", tag=f"bank{bank}")
             for u in range(count):
                 cols = slice(P * (b0 + u), P * (b0 + u + 1))
@@ -216,14 +218,14 @@ def tile_list_federated_client_updates_kernel(
             else:
                 nc.vector.tensor_scalar(result, y, step_col, drift_col, ALU.mult, ALU.add)
 
-        def store_tile(y, u, b, j0, width, on_scalar):
+        def store_tile(y, b, j0, width, on_scalar):
             result = held.tile([P, width], F32, name=f"single{b}_{j0}")
-            finish(result[:], y[:, u, :], b, on_scalar)
+            finish(result[:], y[:, 0, :], b, on_scalar)
             nc.sync.dma_start(out[P * b : P * (b + 1), j0 : j0 + width], result[:])
 
         def expand(b0, j0, width, bank, on_scalar):
-            y = multiply(b0, j0, width, bank)
             count = BLOCK // width
+            y = multiply(b0, count, j0, width, bank)
             result = held.tile([P, count, width], F32, name=f"result{b0}_{j0}")
             for u in range(count):
                 finish(result[:, u, :], y[:, u, :], b0 + u, on_scalar)
@@ -233,22 +235,28 @@ def tile_list_federated_client_updates_kernel(
         bound(0, CHUNK)
         bound(CHUNK, CHUNK)
         weave(0, 0, CHUNK)
-        weave(CHUNK, 0, CHUNK // 4)
-        quantize_h(0, CHUNK)
-        weave(CHUNK, CHUNK // 4, CHUNK)
-        first_y = multiply(0, 0, CHUNK, 7)
-        store_tile(first_y, 0, 0, 0, CHUNK, False)
-        quantize_h(CHUNK, CHUNK)
-        store_tile(first_y, 1, 1, 0, CHUNK, False)
+        weave(CHUNK, 0, COVER)
+        quantize_h(0, 0, CHUNK)
+        store_tile(multiply(2, 1, 0, CHUNK, 1), 2, 0, CHUNK, True)
+        weave(CHUNK, COVER, CHUNK)
+        store_tile(multiply(0, 1, 0, CHUNK, 7), 0, 0, CHUNK, False)
+        store_tile(multiply(3, 1, 0, CHUNK, 3), 3, 0, CHUNK, True)
+        second_y = multiply(1, 1, 0, CHUNK, 2)
+        quantize_h(CHUNK, 0, CHUNK)
+        store_tile(second_y, 1, 0, CHUNK, False)
         for a in range(2):
             first_product(a, 1, PACK - 1, 0)
         bound(BLOCK, BLOCK)
-        expand(2, 0, CHUNK, 1, True)
         weave(BLOCK, 0, BLOCK)
-        quantize_h(BLOCK, BLOCK)
-        for b in range(4, 8):
-            expand(b, 0, BLOCK, (2, 3, 7, 1)[b - 4], True)
-        expand(0, CHUNK, CHUNK, 2, False)
+        quantize_h(BLOCK, 0, BLOCK)
+        halves = held.tile([P, BLOCK], F32, name="halves")
+        for half, bank in enumerate((1, 7)):
+            y_half = multiply(4, 1, CHUNK * half, CHUNK, bank)
+            finish(halves[:, CHUNK * half : CHUNK * (half + 1)], y_half[:, 0, :], 4, True)
+        nc.sync.dma_start(out[P * 4 : P * 5, 0:BLOCK], halves[:])
+        for b in range(5, 8):
+            expand(b, 0, BLOCK, (3, 2, 1)[b - 5], True)
+        expand(0, CHUNK, CHUNK, 7, False)
         expand(2, CHUNK, CHUNK, 3, True)
         for b in range(N_TILES):
             expand(b, BLOCK, BLOCK, (b + 4) % 8, b % 2 == 1)

@@ -19,15 +19,15 @@ ACT = mybir.ActivationFunctionType
 
 P = 128
 PACK = 4
-K_PASS = P * PACK
-BLOCK = 512
+ENTRIES = 512
 N_TILES = N // P
-CAST_SCALAR = (60, 92, 48)
-CHUNK = 256
-COVER = 64
+CHUNK = ENTRIES // 2
 PAIR = 2
 PAIR_BYTES = PAIR * H * 4
+CAST_SCALAR = (60, 92, 48)
+COVER = 64
 WINDOW_OFFSET = PAIR_BYTES - 512
+SPARE_BANK = 7
 
 
 def tile_list_federated_client_updates_kernel(
@@ -62,10 +62,10 @@ def tile_list_federated_client_updates_kernel(
         nc.sync.dma_start(scale_window[0:P:4, :].bitcast(I32), scale_rows)
         load_table(0, T // 2, T)
         nc.sync.dma_start(w1_first[:], w1_rows[0])
-        rows_sb = held.tile([P, P], F32, name="rows_sb")
-        nc.vector.memset(rows_sb[:], 0.0)
-        nc.sync.dma_start(rows_sb[0:N_TILES, :], step.rearrange("(b p) -> b p", p=P))
-        nc.sync.dma_start(rows_sb[N_TILES : 2 * N_TILES, :], drift.rearrange("(b p) -> b p", p=P))
+        vector_rows = held.tile([P, P], F32, name="rows_sb")
+        nc.vector.memset(vector_rows[:], 0.0)
+        nc.sync.dma_start(vector_rows[0:N_TILES, :], step.rearrange("(b p) -> b p", p=P))
+        nc.sync.dma_start(vector_rows[N_TILES : 2 * N_TILES, :], drift.rearrange("(b p) -> b p", p=P))
         load_table(1, 0, T)
 
         ident = held.tile([P, P], F32, name="ident")
@@ -76,16 +76,16 @@ def tile_list_federated_client_updates_kernel(
         nc.gpsimd.dma_start(gain_sb[:], gain.rearrange("(p t) -> p t", t=PACK))
 
         picked_rows = held.tile([P, S], U8, name="picked_rows", align_bytes=64)
-        picked_scales = [held.tile([P, S], U8, name=f"picked_scales{a}", align_bytes=64) for a in range(2)]
+        picked_planes = [held.tile([P, S], U8, name=f"picked_scales{a}", align_bytes=64) for a in range(2)]
         for a in range(2):
-            nc.vector.memset(picked_scales[a][:].bitcast(I32), 0)
+            nc.vector.memset(picked_planes[a][:].bitcast(I32), 0)
         nc.vector.tensor_copy(picked_rows[:], scale_window[:].indirect(offsets[:]))
 
         def move_scale_rows(a):
             for q in range(4):
                 first = 64 * a + 16 * q
                 nc.sync.dma_start(
-                    picked_scales[a][32 * q : 32 * q + 4, :].bitcast(I32),
+                    picked_planes[a][32 * q : 32 * q + 4, :].bitcast(I32),
                     picked_rows[first : first + 16 : 4, :].bitcast(I32),
                 )
 
@@ -94,10 +94,10 @@ def tile_list_federated_client_updates_kernel(
             nc.sync.dma_start(w1_last[u][:], w1_rows[1][:, PAIR * u : PAIR * (u + 1), :])
         move_scale_rows(1)
 
-        turned = psum.tile([P, P], F32, name="turned", tag="bank7")
-        nc.tensor.transpose(turned[:], rows_sb[:], ident[:])
-        cols_sb = held.tile([P, 2 * N_TILES], F32, name="cols_sb")
-        nc.scalar.copy(cols_sb[:], turned[:, 0 : 2 * N_TILES])
+        turned = psum.tile([P, P], F32, name="turned", tag=f"bank{SPARE_BANK}")
+        nc.tensor.transpose(turned[:], vector_rows[:], ident[:])
+        vector_cols = held.tile([P, 2 * N_TILES], F32, name="cols_sb")
+        nc.scalar.copy(vector_cols[:], turned[:, 0 : 2 * N_TILES])
 
         w1_bf = [held.tile([P, PACK * H], BF16, name=f"w1_bf{a}", tag=f"w1_bf{a}", align_bytes=64) for a in range(2)]
         w1_codes = [held.tile([P, H], U32, name=f"w1_codes{a}", align_bytes=64) for a in range(2)]
@@ -116,34 +116,34 @@ def tile_list_federated_client_updates_kernel(
                 w1_codes[a][:, c0:c1].bitcast(E4M3), w1_plane[a][:, c0:c1], w1_bf[a][:, PACK * c0 : PACK * c1]
             )
 
-        def gather_words(a, k, pool, **place):
-            picked[a, k] = pool.tile([P, BLOCK], U32, name=f"picked{a}_{k}", align_bytes=64, **place)
+        def gather_words(a, k, tag):
+            picked[a, k] = held.tile([P, ENTRIES], U32, name=f"picked{a}_{k}", tag=tag, align_bytes=64)
             window = tab[a][:].bitcast(U32)
             nc.vector.tensor_copy(picked[a, k][:], window.indirect(offsets[:, 32 * k : 32 * (k + 1)]))
 
         def first_product(a, k, t, bank):
             if a == 0:
-                acc[k, t] = psum.tile([P, BLOCK], F32, name=f"acc{k}_{t}", tag=f"bank{bank}")
+                acc[k, t] = psum.tile([P, ENTRIES], F32, name=f"acc{k}_{t}", tag=f"bank{bank}")
             cols = slice(P * t, P * (t + 1))
             nc.tensor.matmul_mx(
                 acc[k, t][:],
                 lhsT=w1_codes[a][:, cols].bitcast(E4M3),
                 lhsT_scale=w1_plane[a][:, cols],
                 rhs=picked[a, k][:].bitcast(E5M2),
-                rhs_scale=picked_scales[a][:, BLOCK * k : BLOCK * (k + 1)],
+                rhs_scale=picked_planes[a][:, ENTRIES * k : ENTRIES * (k + 1)],
                 start=a == 0,
                 stop=a == 1,
             )
 
-        gather_words(0, 0, held)
+        gather_words(0, 0, "picked0_0")
         cast_w1(0, w1_first, 0, PACK, CAST_SCALAR[0])
         quantize_w1(0, 0, H)
         for t in range(PACK):
             first_product(0, 0, t, t)
-        gather_words(0, 1, held, tag="w1_bf0")
+        gather_words(0, 1, "w1_bf0")
         for t in range(PACK - 1):
             first_product(0, 1, t, PACK + t)
-        gather_words(1, 0, held)
+        gather_words(1, 0, "picked1_0")
 
         w2_codes = held.tile([P, N], I32, name="w2_codes", tag="w1_first", align_bytes=64)
         nc.sync.dma_start(w2_codes[:], w2_words[0].rearrange("p c i -> p (c i)").bitcast(I32))
@@ -161,17 +161,17 @@ def tile_list_federated_client_updates_kernel(
             quantize_w1(1, P * t, P * (t + 1))
         for t in range(PACK):
             first_product(1, 0, t, t)
-        gather_words(1, 1, held, tag="w1_bf1")
+        gather_words(1, 1, "w1_bf1")
         for t in range(PACK - 1):
             first_product(1, 1, t, PACK + t)
 
         h_plane = held.tile([P, S], U8, name="h_plane", align_bytes=64)
         bounded = {}
         h_bf = {}
-        h_codes = [held.tile([P, BLOCK], U32, name=f"h_codes{k}", align_bytes=64) for k in range(2)]
+        h_codes = [held.tile([P, ENTRIES], U32, name=f"h_codes{k}", align_bytes=64) for k in range(2)]
 
         def bound(j0, width):
-            k, lo = divmod(j0, BLOCK)
+            k, lo = divmod(j0, ENTRIES)
             bounded[j0] = held.tile([P, PACK, width], F32, name=f"bounded{j0}")
             h_bf[j0] = held.tile([P, PACK * width], BF16, name=f"h_bf{j0}", align_bytes=64)
             for t in range(PACK):
@@ -181,21 +181,19 @@ def tile_list_federated_client_updates_kernel(
 
         def weave(j0, c0, c1):
             woven = h_bf[j0][:].rearrange("p (c i t) -> p c t i", i=4, t=PACK)
-            planes = bounded[j0][:].rearrange("p t (c i) -> p c t i", i=4)
+            by_slice = bounded[j0][:].rearrange("p t (c i) -> p c t i", i=4)
             groups = slice(c0 // 4, c1 // 4)
             spread = gain_sb[:].unsqueeze(1).unsqueeze(3).to_broadcast([P, (c1 - c0) // 4, PACK, 4])
-            nc.vector.tensor_tensor(woven[:, groups], planes[:, groups], spread, ALU.mult)
+            nc.vector.tensor_tensor(woven[:, groups], by_slice[:, groups], spread, ALU.mult)
 
-        def quantize_h(j0, c0, c1):
-            k, lo = divmod(j0, BLOCK)
+        def quantize_h(j0, width):
+            k, lo = divmod(j0, ENTRIES)
             nc.vector.quantize_mx(
-                h_codes[k][:, lo + c0 : lo + c1].bitcast(E4M3),
-                h_plane[:, j0 + c0 : j0 + c1],
-                h_bf[j0][:, PACK * c0 : PACK * c1],
+                h_codes[k][:, lo : lo + width].bitcast(E4M3), h_plane[:, j0 : j0 + width], h_bf[j0][:]
             )
 
         def multiply(b0, count, j0, width, bank):
-            k, lo = divmod(j0, BLOCK)
+            k, lo = divmod(j0, ENTRIES)
             y = psum.tile([P, count, width], F32, name=f"y{b0}_{j0}", tag=f"bank{bank}")
             for u in range(count):
                 cols = slice(P * (b0 + u), P * (b0 + u + 1))
@@ -211,20 +209,21 @@ def tile_list_federated_client_updates_kernel(
             return y
 
         def finish(result, y, b, on_scalar):
-            step_col = cols_sb[:, b : b + 1]
-            drift_col = cols_sb[:, N_TILES + b : N_TILES + b + 1]
+            step_col = vector_cols[:, b : b + 1]
+            drift_col = vector_cols[:, N_TILES + b : N_TILES + b + 1]
             if on_scalar:
                 nc.scalar.activation(result, y, ACT.Identity, bias=drift_col, scale=step_col)
             else:
                 nc.vector.tensor_scalar(result, y, step_col, drift_col, ALU.mult, ALU.add)
 
-        def store_tile(y, b, j0, width, on_scalar):
-            result = held.tile([P, width], F32, name=f"single{b}_{j0}")
+        def first_chunk_tile(b, bank, on_scalar):
+            y = multiply(b, 1, 0, CHUNK, bank)
+            result = held.tile([P, CHUNK], F32, name=f"single{b}_0")
             finish(result[:], y[:, 0, :], b, on_scalar)
-            nc.sync.dma_start(out[P * b : P * (b + 1), j0 : j0 + width], result[:])
+            nc.sync.dma_start(out[P * b : P * (b + 1), 0:CHUNK], result[:])
 
         def expand(b0, j0, width, bank, on_scalar):
-            count = BLOCK // width
+            count = ENTRIES // width
             y = multiply(b0, count, j0, width, bank)
             result = held.tile([P, count, width], F32, name=f"result{b0}_{j0}")
             for u in range(count):
@@ -236,27 +235,33 @@ def tile_list_federated_client_updates_kernel(
         bound(CHUNK, CHUNK)
         weave(0, 0, CHUNK)
         weave(CHUNK, 0, COVER)
-        quantize_h(0, 0, CHUNK)
-        store_tile(multiply(2, 1, 0, CHUNK, 1), 2, 0, CHUNK, True)
+        quantize_h(0, CHUNK)
         weave(CHUNK, COVER, CHUNK)
-        store_tile(multiply(0, 1, 0, CHUNK, 7), 0, 0, CHUNK, False)
-        store_tile(multiply(3, 1, 0, CHUNK, 3), 3, 0, CHUNK, True)
-        second_y = multiply(1, 1, 0, CHUNK, 2)
-        quantize_h(CHUNK, 0, CHUNK)
-        store_tile(second_y, 1, 0, CHUNK, False)
+        first_chunk_tile(0, SPARE_BANK, False)
+        quantize_h(CHUNK, CHUNK)
+
         for a in range(2):
             first_product(a, 1, PACK - 1, 0)
-        bound(BLOCK, BLOCK)
-        weave(BLOCK, 0, BLOCK)
-        quantize_h(BLOCK, 0, BLOCK)
-        halves = held.tile([P, BLOCK], F32, name="halves")
-        for half, bank in enumerate((1, 7)):
+        bound(ENTRIES, ENTRIES)
+        for b in range(1, 4):
+            first_chunk_tile(b, b, True)
+        weave(ENTRIES, 0, ENTRIES)
+
+        halves = held.tile([P, ENTRIES], F32, name="halves")
+        for half, bank in enumerate((1, SPARE_BANK)):
             y_half = multiply(4, 1, CHUNK * half, CHUNK, bank)
             finish(halves[:, CHUNK * half : CHUNK * (half + 1)], y_half[:, 0, :], 4, True)
-        nc.sync.dma_start(out[P * 4 : P * 5, 0:BLOCK], halves[:])
-        for b in range(5, 8):
-            expand(b, 0, BLOCK, (3, 2, 1)[b - 5], True)
-        expand(0, CHUNK, CHUNK, 7, False)
-        expand(2, CHUNK, CHUNK, 3, True)
+        nc.sync.dma_start(out[P * 4 : P * 5, 0:ENTRIES], halves[:])
+
+        pair = held.tile([P, 2, CHUNK], F32, name="pair")
+        pair_y = multiply(0, 2, CHUNK, CHUNK, SPARE_BANK)
+        finish(pair[:, 0, :], pair_y[:, 0, :], 0, False)
+        quantize_h(ENTRIES, ENTRIES)
+        finish(pair[:, 1, :], pair_y[:, 1, :], 1, False)
+        for b in range(5, N_TILES):
+            expand(b, 0, ENTRIES, 1 + (b - 4) % 3, True)
+        expand(2, CHUNK, CHUNK, 2, True)
+        nc.sync.dma_start(out[0 : 2 * P, CHUNK:ENTRIES].rearrange("(u p) j -> p u j", p=P), pair[:])
+
         for b in range(N_TILES):
-            expand(b, BLOCK, BLOCK, (b + 4) % 8, b % 2 == 1)
+            expand(b, ENTRIES, ENTRIES, (b + PACK) % N_TILES, b % 2 == 1)

@@ -263,5 +263,11 @@ def tile_list_federated_client_updates_kernel(
         expand(2, CHUNK, CHUNK, 2, True)
         nc.sync.dma_start(out[0 : 2 * P, CHUNK:ENTRIES].rearrange("(u p) j -> p u j", p=P), pair[:])
 
-        for b in range(N_TILES):
-            expand(b, ENTRIES, ENTRIES, (b + PACK) % N_TILES, b % 2 == 1)
+        for b0, count in ((0, 2), (2, 2), (4, 4)):
+            group = held.tile([P, count, ENTRIES], F32, name=f"group{b0}")
+            for u in range(count):
+                b = b0 + u
+                y = multiply(b, 1, ENTRIES, ENTRIES, (b + PACK) % N_TILES)
+                finish(group[:, u, :], y[:, 0, :], b, b % 2 == 1)
+            rows = out[P * b0 : P * (b0 + count), ENTRIES:S].rearrange("(u p) j -> p u j", p=P)
+            nc.sync.dma_start(rows, group[:])

@@ -77,8 +77,6 @@ def tile_list_federated_client_updates_kernel(
 
         picked_rows = held.tile([P, S], U8, name="picked_rows", align_bytes=64)
         picked_planes = [held.tile([P, S], U8, name=f"picked_scales{a}", align_bytes=64) for a in range(2)]
-        for a in range(2):
-            nc.vector.memset(picked_planes[a][:].bitcast(I32), 0)
         nc.vector.tensor_copy(picked_rows[:], scale_window[:].indirect(offsets[:]))
 
         def move_scale_rows(a):
@@ -148,7 +146,6 @@ def tile_list_federated_client_updates_kernel(
         w2_codes = held.tile([P, N], I32, name="w2_codes", tag="w1_first", align_bytes=64)
         nc.sync.dma_start(w2_codes[:], w2_words[0].rearrange("p c i -> p (c i)").bitcast(I32))
         w2_plane = shared.tile([P, N], U8, name="w2_plane", offset=PAIR_BYTES, align_bytes=64)
-        nc.vector.memset(w2_plane[:].bitcast(I32), 0)
         for q in range(4):
             nc.sync.dma_start(
                 w2_plane[32 * q : 32 * q + 4, :].bitcast(I32),

@@ -240,8 +240,11 @@ def tile_list_federated_client_updates_kernel(
         for a in range(2):
             first_product(a, 1, PACK - 1, 0)
         bound(ENTRIES, ENTRIES)
-        for b in range(1, 4):
-            first_chunk_tile(b, b, True)
+        first_chunk_tile(1, 1, True)
+        two = held.tile([P, 2, CHUNK], F32, name="two")
+        for b in (2, 3):
+            finish(two[:, b - 2, :], multiply(b, 1, 0, CHUNK, b)[:, 0, :], b, True)
+        nc.sync.dma_start(out[2 * P : 4 * P, 0:CHUNK].rearrange("(u p) j -> p u j", p=P), two[:])
         weave(ENTRIES, 0, ENTRIES)
 
         halves = held.tile([P, ENTRIES], F32, name="halves")
@@ -260,7 +263,7 @@ def tile_list_federated_client_updates_kernel(
         expand(2, CHUNK, CHUNK, 2, True)
         nc.sync.dma_start(out[0 : 2 * P, CHUNK:ENTRIES].rearrange("(u p) j -> p u j", p=P), pair[:])
 
-        for b0, count in ((0, 2), (2, 2), (4, 4)):
+        for b0, count in ((0, 1), (1, 2), (3, 2), (5, 3)):
             group = held.tile([P, count, ENTRIES], F32, name=f"group{b0}")
             for u in range(count):
                 b = b0 + u

@@ -24,7 +24,7 @@ N_TILES = N // P
 CHUNK = ENTRIES // 2
 PAIR = 2
 PAIR_BYTES = PAIR * H * 4
-CAST_SCALAR = (60, 92, 48)
+CAST_SCALAR = (60, 76, 44)
 COVER = 64
 WINDOW_OFFSET = PAIR_BYTES - 512
 SPARE_BANK = 7

@@ -22,9 +22,9 @@ PACK = 4
 ENTRIES = 512
 N_TILES = N // P
 CHUNK = ENTRIES // 2
-PAIR = 2
-PAIR_BYTES = PAIR * H * 4
-CAST_SCALAR = (60, 76, 44)
+HALF = H // 2
+PAIR_BYTES = PACK * HALF * 4
+CAST_SCALAR = (60, 40, 26)
 COVER = 64
 WINDOW_OFFSET = PAIR_BYTES - 512
 SPARE_BANK = 7
@@ -43,7 +43,7 @@ def tile_list_federated_client_updates_kernel(
 
         w1_first = held.tile([P, PACK, H], F32, name="w1_first", tag="w1_first", align_bytes=64)
         w1_last = [
-            shared.tile([P, PAIR, H], F32, name=f"w1_last{u}", offset=u * (PAIR_BYTES + N), align_bytes=64)
+            shared.tile([P, PACK, HALF], F32, name=f"w1_last{u}", offset=u * (PAIR_BYTES + N), align_bytes=64)
             for u in range(2)
         ]
         tab = [held.tile([P, T], I32, name=f"tab{a}", tag=f"tab{a}", align_bytes=64) for a in range(2)]
@@ -89,7 +89,7 @@ def tile_list_federated_client_updates_kernel(
 
         move_scale_rows(0)
         for u in range(2):
-            nc.sync.dma_start(w1_last[u][:], w1_rows[1][:, PAIR * u : PAIR * (u + 1), :])
+            nc.sync.dma_start(w1_last[u][:], w1_rows[1][:, :, HALF * u : HALF * (u + 1)])
         move_scale_rows(1)
 
         turned = psum.tile([P, P], F32, name="turned", tag=f"bank{SPARE_BANK}")
@@ -103,11 +103,11 @@ def tile_list_federated_client_updates_kernel(
         picked = {}
         acc = {}
 
-        def cast_w1(a, raw, j0, j1, split):
-            dst = w1_bf[a][:].rearrange("p (t m j) -> p m j t", t=PACK, j=PACK)[:, :, j0:j1]
+        def cast_w1(a, raw, m0, m1, split):
+            dst = w1_bf[a][:].rearrange("p (t m j) -> p m j t", t=PACK, j=PACK)[:, m0:m1]
             src = raw[:].rearrange("p j (m t) -> p m j t", t=PACK)
             nc.scalar.copy(dst[:, 0:split], src[:, 0:split])
-            nc.vector.tensor_copy(dst[:, split:P], src[:, split:P])
+            nc.vector.tensor_copy(dst[:, split:], src[:, split:])
 
         def quantize_w1(a, c0, c1):
             nc.vector.quantize_mx(
@@ -134,7 +134,7 @@ def tile_list_federated_client_updates_kernel(
             )
 
         gather_words(0, 0, "picked0_0")
-        cast_w1(0, w1_first, 0, PACK, CAST_SCALAR[0])
+        cast_w1(0, w1_first, 0, P, CAST_SCALAR[0])
         quantize_w1(0, 0, H)
         for t in range(PACK):
             first_product(0, 0, t, t)
@@ -153,7 +153,7 @@ def tile_list_federated_client_updates_kernel(
             )
 
         for u in range(2):
-            cast_w1(1, w1_last[u], PAIR * u, PAIR * (u + 1), CAST_SCALAR[1 + u])
+            cast_w1(1, w1_last[u], P // 2 * u, P // 2 * (u + 1), CAST_SCALAR[1 + u])
         for t in range(PACK):
             quantize_w1(1, P * t, P * (t + 1))
         for t in range(PACK):

@@ -22,11 +22,11 @@ PACK = 4
 ENTRIES = 512
 N_TILES = N // P
 CHUNK = ENTRIES // 2
-HALF = H // 2
-PAIR_BYTES = PACK * HALF * 4
-CAST_SCALAR = (60, 40, 26)
+PASS_BYTES = PACK * H * 4
+CUTS = (0, 64, 96, 128)
+CAST_SCALAR = (60, 32, 12, 12)
 COVER = 64
-WINDOW_OFFSET = PAIR_BYTES - 512
+WINDOW_OFFSET = PASS_BYTES - N
 SPARE_BANK = 7
 
 
@@ -42,10 +42,9 @@ def tile_list_federated_client_updates_kernel(
         offsets = held.tile([P, S // 16], U16, name="offsets")
 
         w1_first = held.tile([P, PACK, H], F32, name="w1_first", tag="w1_first", align_bytes=64)
-        w1_last = [
-            shared.tile([P, PACK, HALF], F32, name=f"w1_last{u}", offset=u * (PAIR_BYTES + N), align_bytes=64)
-            for u in range(2)
-        ]
+        w1_pieces = shared.tile([P, PACK * H], F32, name="w1_pieces", offset=0, align_bytes=64)
+        pieces = list(zip(CUTS, CUTS[1:]))
+        w1_last = [w1_pieces[:, 16 * m0 : 16 * m1].rearrange("p (j c) -> p j c", j=PACK) for m0, m1 in pieces]
         tab = [held.tile([P, T], I32, name=f"tab{a}", tag=f"tab{a}", align_bytes=64) for a in range(2)]
 
         w1_rows = w1.rearrange("(a p j) c -> a p j c", p=P, j=PACK)
@@ -88,8 +87,8 @@ def tile_list_federated_client_updates_kernel(
                 )
 
         move_scale_rows(0)
-        for u in range(2):
-            nc.sync.dma_start(w1_last[u][:], w1_rows[1][:, :, HALF * u : HALF * (u + 1)])
+        for raw, (m0, m1) in zip(w1_last, pieces):
+            nc.sync.dma_start(raw, w1_rows[1][:, :, PACK * m0 : PACK * m1])
         move_scale_rows(1)
 
         turned = psum.tile([P, P], F32, name="turned", tag=f"bank{SPARE_BANK}")
@@ -105,7 +104,7 @@ def tile_list_federated_client_updates_kernel(
 
         def cast_w1(a, raw, m0, m1, split):
             dst = w1_bf[a][:].rearrange("p (t m j) -> p m j t", t=PACK, j=PACK)[:, m0:m1]
-            src = raw[:].rearrange("p j (m t) -> p m j t", t=PACK)
+            src = raw.rearrange("p j (m t) -> p m j t", t=PACK)
             nc.scalar.copy(dst[:, 0:split], src[:, 0:split])
             nc.vector.tensor_copy(dst[:, split:], src[:, split:])
 
@@ -120,7 +119,8 @@ def tile_list_federated_client_updates_kernel(
             nc.vector.tensor_copy(picked[a, k][:], window.indirect(offsets[:, 32 * k : 32 * (k + 1)]))
 
         def first_product(a, k, t, bank):
-            if a == 0:
+            opens = a == k
+            if opens:
                 acc[k, t] = psum.tile([P, ENTRIES], F32, name=f"acc{k}_{t}", tag=f"bank{bank}")
             cols = slice(P * t, P * (t + 1))
             nc.tensor.matmul_mx(
@@ -129,38 +129,37 @@ def tile_list_federated_client_updates_kernel(
                 lhsT_scale=w1_plane[a][:, cols],
                 rhs=picked[a, k][:].bitcast(E5M2),
                 rhs_scale=picked_planes[a][:, ENTRIES * k : ENTRIES * (k + 1)],
-                start=a == 0,
-                stop=a == 1,
+                start=opens,
+                stop=not opens,
             )
 
         gather_words(0, 0, "picked0_0")
-        cast_w1(0, w1_first, 0, P, CAST_SCALAR[0])
+        cast_w1(0, w1_first[:], 0, P, CAST_SCALAR[0])
         quantize_w1(0, 0, H)
         for t in range(PACK):
             first_product(0, 0, t, t)
         gather_words(0, 1, "w1_bf0")
-        for t in range(PACK - 1):
-            first_product(0, 1, t, PACK + t)
         gather_words(1, 0, "picked1_0")
 
         w2_codes = held.tile([P, N], I32, name="w2_codes", tag="w1_first", align_bytes=64)
         nc.sync.dma_start(w2_codes[:], w2_words[0].rearrange("p c i -> p (c i)").bitcast(I32))
-        w2_plane = shared.tile([P, N], U8, name="w2_plane", offset=PAIR_BYTES, align_bytes=64)
+        w2_plane = shared.tile([P, N], U8, name="w2_plane", offset=PASS_BYTES, align_bytes=64)
         for q in range(4):
             nc.sync.dma_start(
                 w2_plane[32 * q : 32 * q + 4, :].bitcast(I32),
                 w2_scales[0, 4 * q : 4 * q + 4, :].bitcast(I32),
             )
 
-        for u in range(2):
-            cast_w1(1, w1_last[u], P // 2 * u, P // 2 * (u + 1), CAST_SCALAR[1 + u])
+        for u, (m0, m1) in enumerate(pieces):
+            cast_w1(1, w1_last[u], m0, m1, CAST_SCALAR[1 + u])
         for t in range(PACK):
             quantize_w1(1, P * t, P * (t + 1))
         for t in range(PACK):
             first_product(1, 0, t, t)
         gather_words(1, 1, "w1_bf1")
         for t in range(PACK - 1):
-            first_product(1, 1, t, PACK + t)
+            for a in (1, 0):
+                first_product(a, 1, t, PACK + t)
 
         h_plane = held.tile([P, S], U8, name="h_plane", align_bytes=64)
         bounded = {}
@@ -237,7 +236,7 @@ def tile_list_federated_client_updates_kernel(
         first_chunk_tile(0, SPARE_BANK, False)
         quantize_h(CHUNK, CHUNK)
 
-        for a in range(2):
+        for a in (1, 0):
             first_product(a, 1, PACK - 1, 0)
         bound(ENTRIES, ENTRIES)
         first_chunk_tile(1, 1, True)

@@ -118,17 +118,18 @@ def tile_list_federated_client_updates_kernel(
             window = tab[a][:].bitcast(U32)
             nc.vector.tensor_copy(picked[a, k][:], window.indirect(offsets[:, 32 * k : 32 * (k + 1)]))
 
-        def first_product(a, k, t, bank):
+        def first_product(a, j0, width, t, bank):
+            k, lo = divmod(j0, ENTRIES)
             opens = a == k
             if opens:
-                acc[k, t] = psum.tile([P, ENTRIES], F32, name=f"acc{k}_{t}", tag=f"bank{bank}")
+                acc[j0, t] = psum.tile([P, width], F32, name=f"acc{j0}_{t}", tag=f"bank{bank}")
             cols = slice(P * t, P * (t + 1))
             nc.tensor.matmul_mx(
-                acc[k, t][:],
+                acc[j0, t][:],
                 lhsT=w1_codes[a][:, cols].bitcast(E4M3),
                 lhsT_scale=w1_plane[a][:, cols],
-                rhs=picked[a, k][:].bitcast(E5M2),
-                rhs_scale=picked_planes[a][:, ENTRIES * k : ENTRIES * (k + 1)],
+                rhs=picked[a, k][:, lo : lo + width].bitcast(E5M2),
+                rhs_scale=picked_planes[a][:, j0 : j0 + width],
                 start=opens,
                 stop=not opens,
             )
@@ -136,8 +137,9 @@ def tile_list_federated_client_updates_kernel(
         gather_words(0, 0, "picked0_0")
         cast_w1(0, w1_first[:], 0, P, CAST_SCALAR[0])
         quantize_w1(0, 0, H)
-        for t in range(PACK):
-            first_product(0, 0, t, t)
+        for c in range(2):
+            for t in range(PACK):
+                first_product(0, CHUNK * c, CHUNK, t, PACK * c + t)
         gather_words(0, 1, "w1_bf0")
         gather_words(1, 0, "picked1_0")
 
@@ -154,12 +156,10 @@ def tile_list_federated_client_updates_kernel(
             cast_w1(1, w1_last[u], m0, m1, CAST_SCALAR[1 + u])
         for t in range(PACK):
             quantize_w1(1, P * t, P * (t + 1))
-        for t in range(PACK):
-            first_product(1, 0, t, t)
+        for c in range(2):
+            for t in range(PACK):
+                first_product(1, CHUNK * c, CHUNK, t, PACK * c + t)
         gather_words(1, 1, "w1_bf1")
-        for t in range(PACK - 1):
-            for a in (1, 0):
-                first_product(a, 1, t, PACK + t)
 
         h_plane = held.tile([P, S], U8, name="h_plane", align_bytes=64)
         bounded = {}
@@ -167,12 +167,11 @@ def tile_list_federated_client_updates_kernel(
         h_codes = [held.tile([P, ENTRIES], U32, name=f"h_codes{k}", align_bytes=64) for k in range(2)]
 
         def bound(j0, width):
-            k, lo = divmod(j0, ENTRIES)
             bounded[j0] = held.tile([P, PACK, width], F32, name=f"bounded{j0}")
             h_bf[j0] = held.tile([P, PACK * width], BF16, name=f"h_bf{j0}", align_bytes=64)
             for t in range(PACK):
                 nc.scalar.activation(
-                    bounded[j0][:, t, :], acc[k, t][:, lo : lo + width], ACT.Tanh, bias=b1_sb[:, t : t + 1]
+                    bounded[j0][:, t, :], acc[j0, t][:], ACT.Tanh, bias=b1_sb[:, t : t + 1]
                 )
 
         def weave(j0, c0, c1):
@@ -228,45 +227,46 @@ def tile_list_federated_client_updates_kernel(
             nc.sync.dma_start(rows, result[:])
 
         bound(0, CHUNK)
+        for t in range(PACK):
+            for a in (1, 0):
+                first_product(a, ENTRIES, ENTRIES, t, t)
         bound(CHUNK, CHUNK)
         weave(0, 0, CHUNK)
         weave(CHUNK, 0, COVER)
         quantize_h(0, CHUNK)
         weave(CHUNK, COVER, CHUNK)
-        first_chunk_tile(0, SPARE_BANK, False)
+        first_chunk_tile(0, 4, False)
         quantize_h(CHUNK, CHUNK)
 
-        for a in (1, 0):
-            first_product(a, 1, PACK - 1, 0)
         bound(ENTRIES, ENTRIES)
-        first_chunk_tile(1, 1, True)
+        first_chunk_tile(1, 5, True)
         two = held.tile([P, 2, CHUNK], F32, name="two")
         for b in (2, 3):
-            finish(two[:, b - 2, :], multiply(b, 1, 0, CHUNK, b)[:, 0, :], b, True)
+            finish(two[:, b - 2, :], multiply(b, 1, 0, CHUNK, PACK + b)[:, 0, :], b, True)
         nc.sync.dma_start(out[2 * P : 4 * P, 0:CHUNK].rearrange("(u p) j -> p u j", p=P), two[:])
         weave(ENTRIES, 0, ENTRIES)
 
         halves = held.tile([P, ENTRIES], F32, name="halves")
-        for half, bank in enumerate((1, SPARE_BANK)):
+        for half, bank in enumerate((5, 4)):
             y_half = multiply(4, 1, CHUNK * half, CHUNK, bank)
             finish(halves[:, CHUNK * half : CHUNK * (half + 1)], y_half[:, 0, :], 4, True)
         nc.sync.dma_start(out[P * 4 : P * 5, 0:ENTRIES], halves[:])
 
         pair = held.tile([P, 2, CHUNK], F32, name="pair")
-        pair_y = multiply(0, 2, CHUNK, CHUNK, SPARE_BANK)
+        pair_y = multiply(0, 2, CHUNK, CHUNK, 4)
         finish(pair[:, 0, :], pair_y[:, 0, :], 0, False)
         quantize_h(ENTRIES, ENTRIES)
         finish(pair[:, 1, :], pair_y[:, 1, :], 1, False)
         for b in range(5, N_TILES):
-            expand(b, 0, ENTRIES, 1 + (b - 4) % 3, True)
-        expand(2, CHUNK, CHUNK, 2, True)
+            expand(b, 0, ENTRIES, 5 + (b - 4) % 3, True)
+        expand(2, CHUNK, CHUNK, 6, True)
         nc.sync.dma_start(out[0 : 2 * P, CHUNK:ENTRIES].rearrange("(u p) j -> p u j", p=P), pair[:])
 
         for b0, count in ((0, 1), (1, 2), (3, 2), (5, 3)):
             group = held.tile([P, count, ENTRIES], F32, name=f"group{b0}")
             for u in range(count):
                 b = b0 + u
-                y = multiply(b, 1, ENTRIES, ENTRIES, (b + PACK) % N_TILES)
+                y = multiply(b, 1, ENTRIES, ENTRIES, b)
                 finish(group[:, u, :], y[:, 0, :], b, b % 2 == 1)
             rows = out[P * b0 : P * (b0 + count), ENTRIES:S].rearrange("(u p) j -> p u j", p=P)
             nc.sync.dma_start(rows, group[:])

@@ -181,10 +181,12 @@ def tile_list_federated_client_updates_kernel(
             spread = gain_sb[:].unsqueeze(1).unsqueeze(3).to_broadcast([P, (c1 - c0) // 4, PACK, 4])
             nc.vector.tensor_tensor(woven[:, groups], by_slice[:, groups], spread, ALU.mult)
 
-        def quantize_h(j0, width):
+        def quantize_h(j0, c0, c1):
             k, lo = divmod(j0, ENTRIES)
             nc.vector.quantize_mx(
-                h_codes[k][:, lo : lo + width].bitcast(E4M3), h_plane[:, j0 : j0 + width], h_bf[j0][:]
+                h_codes[k][:, lo + c0 : lo + c1].bitcast(E4M3),
+                h_plane[:, j0 + c0 : j0 + c1],
+                h_bf[j0][:, PACK * c0 : PACK * c1],
             )
 
         def multiply(b0, count, j0, width, bank):
@@ -233,10 +235,10 @@ def tile_list_federated_client_updates_kernel(
         bound(CHUNK, CHUNK)
         weave(0, 0, CHUNK)
         weave(CHUNK, 0, COVER)
-        quantize_h(0, CHUNK)
+        quantize_h(0, 0, CHUNK)
         weave(CHUNK, COVER, CHUNK)
         first_chunk_tile(0, 4, False)
-        quantize_h(CHUNK, CHUNK)
+        quantize_h(CHUNK, 0, CHUNK)
 
         bound(ENTRIES, ENTRIES)
         first_chunk_tile(1, 5, True)
@@ -244,7 +246,8 @@ def tile_list_federated_client_updates_kernel(
         for b in (2, 3):
             finish(two[:, b - 2, :], multiply(b, 1, 0, CHUNK, PACK + b)[:, 0, :], b, True)
         nc.sync.dma_start(out[2 * P : 4 * P, 0:CHUNK].rearrange("(u p) j -> p u j", p=P), two[:])
-        weave(ENTRIES, 0, ENTRIES)
+        weave(ENTRIES, 0, CHUNK)
+        weave(ENTRIES, CHUNK, ENTRIES)
 
         halves = held.tile([P, ENTRIES], F32, name="halves")
         for half, bank in enumerate((5, 4)):
@@ -254,12 +257,13 @@ def tile_list_federated_client_updates_kernel(
 
         pair = held.tile([P, 2, CHUNK], F32, name="pair")
         pair_y = multiply(0, 2, CHUNK, CHUNK, 4)
+        quantize_h(ENTRIES, 0, CHUNK)
+        quantize_h(ENTRIES, CHUNK, ENTRIES)
         finish(pair[:, 0, :], pair_y[:, 0, :], 0, False)
-        quantize_h(ENTRIES, ENTRIES)
-        finish(pair[:, 1, :], pair_y[:, 1, :], 1, False)
         for b in range(5, N_TILES):
             expand(b, 0, ENTRIES, 5 + (b - 4) % 3, True)
         expand(2, CHUNK, CHUNK, 6, True)
+        finish(pair[:, 1, :], pair_y[:, 1, :], 1, True)
         nc.sync.dma_start(out[0 : 2 * P, CHUNK:ENTRIES].rearrange("(u p) j -> p u j", p=P), pair[:])
 
         for b0, count in ((0, 1), (1, 2), (3, 2), (5, 3)):

@@ -39,13 +39,13 @@ def tile_list_federated_client_updates_kernel(
         shared = ctx.enter_context(tc.tile_pool(name="shared", bufs=1))
         psum = ctx.enter_context(tc.psum_pool(name="psum", bufs=1))
 
-        offsets = held.tile([P, S // 16], U16, name="offsets")
+        offsets = held.tile([P, S // 16], U16, name="offsets", align_bytes=256)
 
-        w1_first = held.tile([P, PACK, H], F32, name="w1_first", tag="w1_first", align_bytes=64)
-        w1_pieces = shared.tile([P, PACK * H], F32, name="w1_pieces", offset=0, align_bytes=64)
+        w1_first = held.tile([P, PACK, H], F32, name="w1_first", tag="w1_first", align_bytes=256)
+        w1_pieces = shared.tile([P, PACK * H], F32, name="w1_pieces", offset=0, align_bytes=256)
         pieces = list(zip(CUTS, CUTS[1:]))
         w1_last = [w1_pieces[:, 16 * m0 : 16 * m1].rearrange("p (j c) -> p j c", j=PACK) for m0, m1 in pieces]
-        tab = [held.tile([P, T], I32, name=f"tab{a}", tag=f"tab{a}", align_bytes=64) for a in range(2)]
+        tab = [held.tile([P, T], I32, name=f"tab{a}", tag=f"tab{a}", align_bytes=256) for a in range(2)]
 
         w1_rows = w1.rearrange("(a p j) c -> a p j c", p=P, j=PACK)
 
@@ -55,27 +55,27 @@ def tile_list_federated_client_updates_kernel(
 
         load_table(0, 0, T // 2)
         nc.sync.dma_start(offsets[:], offs)
-        scale_window = shared.tile([P, T], U8, name="scale_window", offset=WINDOW_OFFSET, align_bytes=64)
+        scale_window = shared.tile([P, T], U8, name="scale_window", offset=WINDOW_OFFSET, align_bytes=256)
         nc.gpsimd.memset(scale_window[:].bitcast(I32), 0)
         scale_rows = tab_scales.rearrange("a q t -> (a q) t").bitcast(I32)
         nc.sync.dma_start(scale_window[0:P:4, :].bitcast(I32), scale_rows)
         load_table(0, T // 2, T)
         nc.sync.dma_start(w1_first[:], w1_rows[0])
-        vector_rows = held.tile([P, P], F32, name="rows_sb")
+        vector_rows = held.tile([P, P], F32, name="rows_sb", align_bytes=256)
         nc.vector.memset(vector_rows[:], 0.0)
         nc.sync.dma_start(vector_rows[0:N_TILES, :], step.rearrange("(b p) -> b p", p=P))
         nc.sync.dma_start(vector_rows[N_TILES : 2 * N_TILES, :], drift.rearrange("(b p) -> b p", p=P))
         load_table(1, 0, T)
 
-        ident = held.tile([P, P], F32, name="ident")
+        ident = held.tile([P, P], F32, name="ident", align_bytes=256)
         make_identity(nc, ident[:])
-        b1_sb = held.tile([P, PACK], F32, name="b1_sb")
-        gain_sb = held.tile([P, PACK], F32, name="gain_sb")
+        b1_sb = held.tile([P, PACK], F32, name="b1_sb", align_bytes=256)
+        gain_sb = held.tile([P, PACK], F32, name="gain_sb", align_bytes=256)
         nc.gpsimd.dma_start(b1_sb[:], b1.rearrange("(p t) -> p t", t=PACK))
         nc.gpsimd.dma_start(gain_sb[:], gain.rearrange("(p t) -> p t", t=PACK))
 
-        picked_rows = held.tile([P, S], U8, name="picked_rows", align_bytes=64)
-        picked_planes = [held.tile([P, S], U8, name=f"picked_scales{a}", align_bytes=64) for a in range(2)]
+        picked_rows = held.tile([P, S], U8, name="picked_rows", align_bytes=256)
+        picked_planes = [held.tile([P, S], U8, name=f"picked_scales{a}", align_bytes=256) for a in range(2)]
         nc.vector.tensor_copy(picked_rows[:], scale_window[:].indirect(offsets[:]))
 
         def move_scale_rows(a):
@@ -93,12 +93,12 @@ def tile_list_federated_client_updates_kernel(
 
         turned = psum.tile([P, P], F32, name="turned", tag=f"bank{SPARE_BANK}")
         nc.tensor.transpose(turned[:], vector_rows[:], ident[:])
-        vector_cols = held.tile([P, 2 * N_TILES], F32, name="cols_sb")
+        vector_cols = held.tile([P, 2 * N_TILES], F32, name="cols_sb", align_bytes=256)
         nc.scalar.copy(vector_cols[:], turned[:, 0 : 2 * N_TILES])
 
-        w1_bf = [held.tile([P, PACK * H], BF16, name=f"w1_bf{a}", tag=f"w1_bf{a}", align_bytes=64) for a in range(2)]
-        w1_codes = [held.tile([P, H], U32, name=f"w1_codes{a}", align_bytes=64) for a in range(2)]
-        w1_plane = [held.tile([P, H], U8, name=f"w1_plane{a}", align_bytes=64) for a in range(2)]
+        w1_bf = [held.tile([P, PACK * H], BF16, name=f"w1_bf{a}", tag=f"w1_bf{a}", align_bytes=256) for a in range(2)]
+        w1_codes = [held.tile([P, H], U32, name=f"w1_codes{a}", align_bytes=256) for a in range(2)]
+        w1_plane = [held.tile([P, H], U8, name=f"w1_plane{a}", align_bytes=256) for a in range(2)]
         picked = {}
         acc = {}
 
@@ -114,7 +114,7 @@ def tile_list_federated_client_updates_kernel(
             )
 
         def gather_words(a, k, tag):
-            picked[a, k] = held.tile([P, ENTRIES], U32, name=f"picked{a}_{k}", tag=tag, align_bytes=64)
+            picked[a, k] = held.tile([P, ENTRIES], U32, name=f"picked{a}_{k}", tag=tag, align_bytes=256)
             window = tab[a][:].bitcast(U32)
             nc.vector.tensor_copy(picked[a, k][:], window.indirect(offsets[:, 32 * k : 32 * (k + 1)]))
 
@@ -143,9 +143,9 @@ def tile_list_federated_client_updates_kernel(
         gather_words(0, 1, "w1_bf0")
         gather_words(1, 0, "picked1_0")
 
-        w2_codes = held.tile([P, N], I32, name="w2_codes", tag="w1_first", align_bytes=64)
+        w2_codes = held.tile([P, N], I32, name="w2_codes", tag="w1_first", align_bytes=256)
         nc.sync.dma_start(w2_codes[:], w2_words[0].rearrange("p c i -> p (c i)").bitcast(I32))
-        w2_plane = shared.tile([P, N], U8, name="w2_plane", offset=PASS_BYTES, align_bytes=64)
+        w2_plane = shared.tile([P, N], U8, name="w2_plane", offset=PASS_BYTES, align_bytes=256)
         for q in range(4):
             nc.sync.dma_start(
                 w2_plane[32 * q : 32 * q + 4, :].bitcast(I32),
@@ -161,14 +161,14 @@ def tile_list_federated_client_updates_kernel(
                 first_product(1, CHUNK * c, CHUNK, t, PACK * c + t)
         gather_words(1, 1, "w1_bf1")
 
-        h_plane = held.tile([P, S], U8, name="h_plane", align_bytes=64)
+        h_plane = held.tile([P, S], U8, name="h_plane", align_bytes=256)
         bounded = {}
         h_bf = {}
-        h_codes = [held.tile([P, ENTRIES], U32, name=f"h_codes{k}", align_bytes=64) for k in range(2)]
+        h_codes = [held.tile([P, ENTRIES], U32, name=f"h_codes{k}", align_bytes=256) for k in range(2)]
 
         def bound(j0, width):
-            bounded[j0] = held.tile([P, PACK, width], F32, name=f"bounded{j0}")
-            h_bf[j0] = held.tile([P, PACK * width], BF16, name=f"h_bf{j0}", align_bytes=64)
+            bounded[j0] = held.tile([P, PACK, width], F32, name=f"bounded{j0}", align_bytes=256)
+            h_bf[j0] = held.tile([P, PACK * width], BF16, name=f"h_bf{j0}", align_bytes=256)
             for t in range(PACK):
                 nc.scalar.activation(
                     bounded[j0][:, t, :], acc[j0, t][:], ACT.Tanh, bias=b1_sb[:, t : t + 1]
@@ -215,14 +215,14 @@ def tile_list_federated_client_updates_kernel(
 
         def first_chunk_tile(b, bank, on_scalar):
             y = multiply(b, 1, 0, CHUNK, bank)
-            result = held.tile([P, CHUNK], F32, name=f"single{b}_0")
+            result = held.tile([P, CHUNK], F32, name=f"single{b}_0", align_bytes=256)
             finish(result[:], y[:, 0, :], b, on_scalar)
             nc.sync.dma_start(out[P * b : P * (b + 1), 0:CHUNK], result[:])
 
         def expand(b0, j0, width, bank, on_scalar):
             count = ENTRIES // width
             y = multiply(b0, count, j0, width, bank)
-            result = held.tile([P, count, width], F32, name=f"result{b0}_{j0}")
+            result = held.tile([P, count, width], F32, name=f"result{b0}_{j0}", align_bytes=256)
             for u in range(count):
                 finish(result[:, u, :], y[:, u, :], b0 + u, on_scalar)
             rows = out[P * b0 : P * (b0 + count), j0 : j0 + width].rearrange("(u p) j -> p u j", p=P)
@@ -242,20 +242,20 @@ def tile_list_federated_client_updates_kernel(
 
         bound(ENTRIES, ENTRIES)
         first_chunk_tile(1, 5, True)
-        two = held.tile([P, 2, CHUNK], F32, name="two")
+        two = held.tile([P, 2, CHUNK], F32, name="two", align_bytes=256)
         for b in (2, 3):
             finish(two[:, b - 2, :], multiply(b, 1, 0, CHUNK, PACK + b)[:, 0, :], b, True)
         nc.sync.dma_start(out[2 * P : 4 * P, 0:CHUNK].rearrange("(u p) j -> p u j", p=P), two[:])
         weave(ENTRIES, 0, CHUNK)
         weave(ENTRIES, CHUNK, ENTRIES)
 
-        halves = held.tile([P, ENTRIES], F32, name="halves")
+        halves = held.tile([P, ENTRIES], F32, name="halves", align_bytes=256)
         for half, bank in enumerate((5, 4)):
             y_half = multiply(4, 1, CHUNK * half, CHUNK, bank)
             finish(halves[:, CHUNK * half : CHUNK * (half + 1)], y_half[:, 0, :], 4, True)
         nc.sync.dma_start(out[P * 4 : P * 5, 0:ENTRIES], halves[:])
 
-        pair = held.tile([P, 2, CHUNK], F32, name="pair")
+        pair = held.tile([P, 2, CHUNK], F32, name="pair", align_bytes=256)
         pair_y = multiply(0, 2, CHUNK, CHUNK, 4)
         quantize_h(ENTRIES, 0, CHUNK)
         quantize_h(ENTRIES, CHUNK, ENTRIES)
@@ -267,7 +267,7 @@ def tile_list_federated_client_updates_kernel(
         nc.sync.dma_start(out[0 : 2 * P, CHUNK:ENTRIES].rearrange("(u p) j -> p u j", p=P), pair[:])
 
         for b0, count in ((0, 1), (1, 2), (3, 2), (5, 3)):
-            group = held.tile([P, count, ENTRIES], F32, name=f"group{b0}")
+            group = held.tile([P, count, ENTRIES], F32, name=f"group{b0}", align_bytes=256)
             for u in range(count):
                 b = b0 + u
                 y = multiply(b, 1, ENTRIES, ENTRIES, b)

from contextlib import ExitStack

import concourse.mybir as mybir
from concourse.masks import make_identity

K, T, S, H, N = 1024, 2048, 1024, 512, 1024
FLOPS = 2 * K * H * S + 2 * H * N * S

F32 = mybir.dt.float32
BF16 = mybir.dt.bfloat16
I32 = mybir.dt.int32
U32 = mybir.dt.uint32
U16 = mybir.dt.uint16
U8 = mybir.dt.uint8
E4M3 = mybir.dt.float8_e4m3fn_x4
E5M2 = mybir.dt.float8_e5m2_x4
ALU = mybir.AluOpType
ACT = mybir.ActivationFunctionType

P = 128
PACK = 4
ENTRIES = 512
N_TILES = N // P
CHUNK = ENTRIES // 2
PASS_BYTES = PACK * H * 4
CUTS = (0, 64, 96, 128)
CAST_SCALAR = (60, 32, 12, 12)
COVER = 64
WINDOW_OFFSET = PASS_BYTES - N
SPARE_BANK = 7


def tile_list_federated_client_updates_kernel(
    tc, tab_words, tab_scales, offs, w1, b1, gain, w2_words, w2_scales, step, drift, out
):
    nc = tc.nc
    with ExitStack() as ctx:
        held = ctx.enter_context(tc.tile_pool(name="held", bufs=1))
        shared = ctx.enter_context(tc.tile_pool(name="shared", bufs=1))
        psum = ctx.enter_context(tc.psum_pool(name="psum", bufs=1))

        offsets = held.tile([P, S // 16], U16, name="offsets", align_bytes=256)

        w1_first = held.tile([P, PACK, H], F32, name="w1_first", tag="w1_first", align_bytes=256)
        w1_pieces = shared.tile([P, PACK * H], F32, name="w1_pieces", offset=0, align_bytes=256)
        pieces = list(zip(CUTS, CUTS[1:]))
        w1_last = [w1_pieces[:, 16 * m0 : 16 * m1].rearrange("p (j c) -> p j c", j=PACK) for m0, m1 in pieces]
        tab = [held.tile([P, T], I32, name=f"tab{a}", tag=f"tab{a}", align_bytes=256) for a in range(2)]

        w1_rows = w1.rearrange("(a p j) c -> a p j c", p=P, j=PACK)

        def load_table(a, t0, t1):
            words = tab_words[a].rearrange("p t i -> p (t i)").bitcast(I32)
            nc.sync.dma_start(tab[a][:, t0:t1], words[:, t0:t1])

        load_table(0, 0, T // 2)
        nc.sync.dma_start(offsets[:], offs)
        scale_window = shared.tile([P, T], U8, name="scale_window", offset=WINDOW_OFFSET, align_bytes=256)
        nc.gpsimd.memset(scale_window[:].bitcast(I32), 0)
        scale_rows = tab_scales.rearrange("a q t -> (a q) t").bitcast(I32)
        nc.sync.dma_start(scale_window[0:P:4, :].bitcast(I32), scale_rows)
        load_table(0, T // 2, T)
        nc.sync.dma_start(w1_first[:], w1_rows[0])
        vector_rows = held.tile([P, P], F32, name="rows_sb", align_bytes=256)
        nc.vector.memset(vector_rows[:], 0.0)
        nc.sync.dma_start(vector_rows[0:N_TILES, :], step.rearrange("(b p) -> b p", p=P))
        nc.sync.dma_start(vector_rows[N_TILES : 2 * N_TILES, :], drift.rearrange("(b p) -> b p", p=P))
        load_table(1, 0, T)

        ident = held.tile([P, P], F32, name="ident", align_bytes=256)
        make_identity(nc, ident[:])
        b1_sb = held.tile([P, PACK], F32, name="b1_sb", align_bytes=256)
        gain_sb = held.tile([P, PACK], F32, name="gain_sb", align_bytes=256)
        nc.gpsimd.dma_start(b1_sb[:], b1.rearrange("(p t) -> p t", t=PACK))
        nc.gpsimd.dma_start(gain_sb[:], gain.rearrange("(p t) -> p t", t=PACK))

        picked_rows = held.tile([P, S], U8, name="picked_rows", align_bytes=256)
        picked_planes = [held.tile([P, S], U8, name=f"picked_scales{a}", align_bytes=256) for a in range(2)]
        nc.vector.tensor_copy(picked_rows[:], scale_window[:].indirect(offsets[:]))

        def move_scale_rows(a):
            for q in range(4):
                first = 64 * a + 16 * q
                nc.sync.dma_start(
                    picked_planes[a][32 * q : 32 * q + 4, :].bitcast(I32),
                    picked_rows[first : first + 16 : 4, :].bitcast(I32),
                )

        move_scale_rows(0)
        for raw, (m0, m1) in zip(w1_last, pieces):
            nc.sync.dma_start(raw, w1_rows[1][:, :, PACK * m0 : PACK * m1])
        move_scale_rows(1)

        turned = psum.tile([P, P], F32, name="turned", tag=f"bank{SPARE_BANK}")
        nc.tensor.transpose(turned[:], vector_rows[:], ident[:])
        vector_cols = held.tile([P, 2 * N_TILES], F32, name="cols_sb", align_bytes=256)
        nc.scalar.copy(vector_cols[:], turned[:, 0 : 2 * N_TILES])

        w1_bf = [held.tile([P, PACK * H], BF16, name=f"w1_bf{a}", tag=f"w1_bf{a}", align_bytes=256) for a in range(2)]
        w1_codes = [held.tile([P, H], U32, name=f"w1_codes{a}", align_bytes=256) for a in range(2)]
        w1_plane = [held.tile([P, H], U8, name=f"w1_plane{a}", align_bytes=256) for a in range(2)]
        picked = {}
        acc = {}

        def cast_w1(a, raw, m0, m1, split):
            dst = w1_bf[a][:].rearrange("p (t m j) -> p m j t", t=PACK, j=PACK)[:, m0:m1]
            src = raw.rearrange("p j (m t) -> p m j t", t=PACK)
            nc.scalar.copy(dst[:, 0:split], src[:, 0:split])
            nc.vector.tensor_copy(dst[:, split:], src[:, split:])

        def quantize_w1(a, c0, c1):
            nc.vector.quantize_mx(
                w1_codes[a][:, c0:c1].bitcast(E4M3), w1_plane[a][:, c0:c1], w1_bf[a][:, PACK * c0 : PACK * c1]
            )

        def gather_words(a, k, tag):
            picked[a, k] = held.tile([P, ENTRIES], U32, name=f"picked{a}_{k}", tag=tag, align_bytes=256)
            window = tab[a][:].bitcast(U32)
            nc.vector.tensor_copy(picked[a, k][:], window.indirect(offsets[:, 32 * k : 32 * (k + 1)]))

        def first_product(a, j0, width, t, bank):
            k, lo = divmod(j0, ENTRIES)
            opens = a == k
            if opens:
                acc[j0, t] = psum.tile([P, width], F32, name=f"acc{j0}_{t}", tag=f"bank{bank}")
            cols = slice(P * t, P * (t + 1))
            nc.tensor.matmul_mx(
                acc[j0, t][:],
                lhsT=w1_codes[a][:, cols].bitcast(E4M3),
                lhsT_scale=w1_plane[a][:, cols],
                rhs=picked[a, k][:, lo : lo + width].bitcast(E5M2),
                rhs_scale=picked_planes[a][:, j0 : j0 + width],
                start=opens,
                stop=not opens,
            )

        gather_words(0, 0, "picked0_0")
        cast_w1(0, w1_first[:], 0, P, CAST_SCALAR[0])
        quantize_w1(0, 0, H)
        for c in range(2):
            for t in range(PACK):
                first_product(0, CHUNK * c, CHUNK, t, PACK * c + t)
        gather_words(0, 1, "w1_bf0")
        gather_words(1, 0, "picked1_0")

        w2_codes = held.tile([P, N], I32, name="w2_codes", tag="w1_first", align_bytes=256)
        nc.sync.dma_start(w2_codes[:], w2_words[0].rearrange("p c i -> p (c i)").bitcast(I32))
        w2_plane = shared.tile([P, N], U8, name="w2_plane", offset=PASS_BYTES, align_bytes=256)
        for q in range(4):
            nc.sync.dma_start(
                w2_plane[32 * q : 32 * q + 4, :].bitcast(I32),
                w2_scales[0, 4 * q : 4 * q + 4, :].bitcast(I32),
            )

        for u, (m0, m1) in enumerate(pieces):
            cast_w1(1, w1_last[u], m0, m1, CAST_SCALAR[1 + u])
        for t in range(PACK):
            quantize_w1(1, P * t, P * (t + 1))
        for c in range(2):
            for t in range(PACK):
                first_product(1, CHUNK * c, CHUNK, t, PACK * c + t)
        gather_words(1, 1, "w1_bf1")

        h_plane = held.tile([P, S], U8, name="h_plane", align_bytes=256)
        bounded = {}
        h_bf = {}
        h_codes = [held.tile([P, ENTRIES], U32, name=f"h_codes{k}", align_bytes=256) for k in range(2)]

        def bound(j0, width):
            bounded[j0] = held.tile([P, PACK, width], F32, name=f"bounded{j0}", align_bytes=256)
            h_bf[j0] = held.tile([P, PACK * width], BF16, name=f"h_bf{j0}", align_bytes=256)
            for t in range(PACK):
                nc.scalar.activation(
                    bounded[j0][:, t, :], acc[j0, t][:], ACT.Tanh, bias=b1_sb[:, t : t + 1]
                )

        def weave(j0, c0, c1):
            woven = h_bf[j0][:].rearrange("p (c i t) -> p c t i", i=4, t=PACK)
            by_slice = bounded[j0][:].rearrange("p t (c i) -> p c t i", i=4)
            groups = slice(c0 // 4, c1 // 4)
            spread = gain_sb[:].unsqueeze(1).unsqueeze(3).to_broadcast([P, (c1 - c0) // 4, PACK, 4])
            nc.vector.tensor_tensor(woven[:, groups], by_slice[:, groups], spread, ALU.mult)

        def quantize_h(j0, c0, c1):
            k, lo = divmod(j0, ENTRIES)
            nc.vector.quantize_mx(
                h_codes[k][:, lo + c0 : lo + c1].bitcast(E4M3),
                h_plane[:, j0 + c0 : j0 + c1],
                h_bf[j0][:, PACK * c0 : PACK * c1],
            )

        def multiply(b0, count, j0, width, bank):
            k, lo = divmod(j0, ENTRIES)
            y = psum.tile([P, count, width], F32, name=f"y{b0}_{j0}", tag=f"bank{bank}")
            for u in range(count):
                cols = slice(P * (b0 + u), P * (b0 + u + 1))
                nc.tensor.matmul_mx(
                    y[:, u, :],
                    lhsT=w2_codes[:, cols].bitcast(E4M3),
                    lhsT_scale=w2_plane[:, cols],
                    rhs=h_codes[k][:, lo : lo + width].bitcast(E4M3),
                    rhs_scale=h_plane[:, j0 : j0 + width],
                    start=True,
                    stop=True,
                )
            return y

        def finish(result, y, b, on_scalar):
            step_col = vector_cols[:, b : b + 1]
            drift_col = vector_cols[:, N_TILES + b : N_TILES + b + 1]
            if on_scalar:
                nc.scalar.activation(result, y, ACT.Identity, bias=drift_col, scale=step_col)
            else:
                nc.vector.tensor_scalar(result, y, step_col, drift_col, ALU.mult, ALU.add)

        def first_chunk_tile(b, bank, on_scalar):
            y = multiply(b, 1, 0, CHUNK, bank)
            result = held.tile([P, CHUNK], F32, name=f"single{b}_0", align_bytes=256)
            finish(result[:], y[:, 0, :], b, on_scalar)
            nc.sync.dma_start(out[P * b : P * (b + 1), 0:CHUNK], result[:])

        def expand(b0, j0, width, bank, on_scalar):
            count = ENTRIES // width
            y = multiply(b0, count, j0, width, bank)
            result = held.tile([P, count, width], F32, name=f"result{b0}_{j0}", align_bytes=256)
            for u in range(count):
                finish(result[:, u, :], y[:, u, :], b0 + u, on_scalar)
            rows = out[P * b0 : P * (b0 + count), j0 : j0 + width].rearrange("(u p) j -> p u j", p=P)
            nc.sync.dma_start(rows, result[:])

        bound(0, CHUNK)
        for t in range(PACK):
            for a in (1, 0):
                first_product(a, ENTRIES, ENTRIES, t, t)
        bound(CHUNK, CHUNK)
        weave(0, 0, CHUNK)
        weave(CHUNK, 0, COVER)
        quantize_h(0, 0, CHUNK)
        weave(CHUNK, COVER, CHUNK)
        first_chunk_tile(0, 4, False)
        quantize_h(CHUNK, 0, CHUNK)

        bound(ENTRIES, ENTRIES)
        first_chunk_tile(1, 5, True)
        two = held.tile([P, 2, CHUNK], F32, name="two", align_bytes=256)
        for b in (2, 3):
            finish(two[:, b - 2, :], multiply(b, 1, 0, CHUNK, PACK + b)[:, 0, :], b, True)
        nc.sync.dma_start(out[2 * P : 4 * P, 0:CHUNK].rearrange("(u p) j -> p u j", p=P), two[:])
        weave(ENTRIES, 0, CHUNK)
        weave(ENTRIES, CHUNK, ENTRIES)

        halves = held.tile([P, ENTRIES], F32, name="halves", align_bytes=256)
        for half, bank in enumerate((5, 4)):
            y_half = multiply(4, 1, CHUNK * half, CHUNK, bank)
            finish(halves[:, CHUNK * half : CHUNK * (half + 1)], y_half[:, 0, :], 4, True)
        nc.sync.dma_start(out[P * 4 : P * 5, 0:ENTRIES], halves[:])

        pair = held.tile([P, 2, CHUNK], F32, name="pair", align_bytes=256)
        pair_y = multiply(0, 2, CHUNK, CHUNK, 4)
        quantize_h(ENTRIES, 0, CHUNK)
        quantize_h(ENTRIES, CHUNK, ENTRIES)
        finish(pair[:, 0, :], pair_y[:, 0, :], 0, False)
        for b in range(5, N_TILES):
            expand(b, 0, ENTRIES, 5 + (b - 4) % 3, True)
        expand(2, CHUNK, CHUNK, 6, True)
        finish(pair[:, 1, :], pair_y[:, 1, :], 1, True)
        nc.sync.dma_start(out[0 : 2 * P, CHUNK:ENTRIES].rearrange("(u p) j -> p u j", p=P), pair[:])

        for b0, count in ((0, 1), (1, 2), (3, 2), (5, 3)):
            group = held.tile([P, count, ENTRIES], F32, name=f"group{b0}", align_bytes=256)
            for u in range(count):
                b = b0 + u
                y = multiply(b, 1, ENTRIES, ENTRIES, b)
                finish(group[:, u, :], y[:, 0, :], b, b % 2 == 1)
            rows = out[P * b0 : P * (b0 + count), ENTRIES:S].rearrange("(u p) j -> p u j", p=P)
            nc.sync.dma_start(rows, group[:])
